import numpy as np
import ml_dtypes


def mxq(x, axis, fmt="e4m3"):
    dtype, down = {"e4m3": (ml_dtypes.float8_e4m3fn, 7), "e5m2": (ml_dtypes.float8_e5m2, 14)}[fmt]
    v = np.moveaxis(np.asarray(x, np.float32).astype(ml_dtypes.bfloat16).astype(np.float64), axis, -1)
    blocks = v.reshape(v.shape[:-1] + (-1, 32))
    amax = np.abs(blocks).max(-1, keepdims=True)
    byte = np.maximum(np.where(amax > 0, np.frexp(amax)[1] - 1 + 127, 0) - down, 1)
    scale = np.exp2(byte - 127.0)
    codes = (blocks / scale).astype(np.float32).astype(dtype).astype(np.float64)
    return np.moveaxis((codes * scale).reshape(v.shape), -1, axis)


WIDE = False


def mx_kscale(k):
    if not WIDE:
        return np.ones(k)
    levels = np.array([10, -10, 5, -5, 0])
    if k % 512:
        return np.exp2(np.random.permutation(np.resize(levels, k // 32))).repeat(32)
    a = np.empty((k // 512, 16))
    for p in range(k // 512):
        a[p, :8] = np.random.permutation(np.resize(levels, 8))
        for g in range(8):
            far = levels[np.abs(levels - a[p, g]) >= 10]
            a[p, g + 8] = far[np.random.randint(len(far))]
    return np.exp2(a.ravel()).repeat(32)


BF16 = ml_dtypes.bfloat16


def bf(x):
    return np.asarray(x, np.float32).astype(BF16)


def f64(x):
    return np.asarray(x).astype(np.float64)

def planes(Y):
    n, m = Y.shape
    b = f64(bf(Y)).reshape(n // 32, 32, m)
    amax = np.abs(b).max(1)
    byte = np.clip(np.where(amax > 0, np.frexp(amax)[1] - 1 + 127 - 7, 1), 1, 254)
    codes = (b * np.exp2(127.0 - byte)[:, None, :]).reshape(n, m).astype(np.float32).astype(ml_dtypes.float8_e4m3fn).view(np.uint8)
    words = codes.reshape(n // 512, 128, 4, m).transpose(0, 1, 3, 2)
    return np.ascontiguousarray(words), np.ascontiguousarray(byte.astype(np.uint8).reshape(n // 512, 16, m))


D, T, P = 1024, 2048, 512


def setup_inputs():
    s = mx_kscale(D)
    q = mx_kscale(P)
    phases = np.random.uniform(-3.0, 3.0, (D, T))
    amp = np.exp(0.3 * np.random.randn(D)) * s
    koopman = 1.2 * np.random.randn(D, D) / np.sqrt(D) / s[None, :]
    control = 0.6 * np.random.randn(D, P) / np.sqrt(P) * q[None, :]
    u = np.random.randn(P, T) / q[:, None]
    drift = 0.3 * np.random.randn(D)
    unit = np.exp(0.8 * np.random.randn(D))
    return {"phases": bf(phases), "amp": bf(amp), "koopman": bf(koopman),
            "control": bf(control), "u": bf(u), "drift": bf(drift), "unit": bf(unit)}

def reference(phases, amp, koopman, control, u, drift, unit):
    psi = np.sin(f64(phases)) * f64(amp)[:, None]
    advanced = mxq(f64(koopman), 1, "e4m3") @ mxq(psi, 0, "e4m3")
    offset = mxq(f64(control), 1, "e4m3") @ mxq(f64(u), 0, "e4m3")
    y = (advanced + offset + f64(drift)[:, None]) * f64(unit)[:, None]
    Y = y.reshape(D, T)
    words, scales = planes(Y)
    return y, words, scales

@@ -1,0 +1,449 @@
+from contextlib import ExitStack
+
+import concourse.mybir as mybir
+from concourse.masks import make_identity
+
+D, T, CH = 1024, 2048, 512
+FLOPS = 2 * D * (D + CH) * T
+
+F32 = mybir.dt.float32
+BF16 = mybir.dt.bfloat16
+U32 = mybir.dt.uint32
+I32 = mybir.dt.int32
+U8 = mybir.dt.uint8
+FP8X4 = mybir.dt.float8_e4m3fn_x4
+ACT = mybir.ActivationFunctionType
+ALU = mybir.AluOpType
+
+P = 128
+PACK = 4
+K_PASS = P * PACK
+GROUPS = D // K_PASS
+PSI_PASSES = D // K_PASS
+U_PASS = PSI_PASSES
+PASSES = PSI_PASSES + 1
+BANKS = 8
+BANK = 512
+WIDTHS = [256, 512, 512, 512, 256]
+STARTS = [sum(WIDTHS[:n]) for n in range(len(WIDTHS))]
+CHUNKS = len(WIDTHS)
+EARLY_CHUNKS = CHUNKS - 1
+SIN_BUFS, PSI_BUFS, U_BUFS, W_BUFS, Y_BUFS, YB_BUFS = 2, 2, 1, 2, 5, 2
+
+ORDER = [
+    ("load_phases", 0, 0),
+    ("prepare",),
+    ("sine", 0, 0),
+    ("load_amp",),
+    ("times_amp", 0, 0),
+    ("load_phases", 0, 1),
+    ("sine", 0, 1),
+    ("load_phases", 1, 0),
+    ("load_weight", 0, 0),
+    ("times_amp", 0, 1),
+    ("load_u", 0),
+    ("load_weight", 0, 1),
+    ("load_phases", 1, 1),
+    ("sine", 1, 0),
+    ("quantize_psi", 0, 0),
+    ("interleave_u", 0, False),
+    ("quantize_psi", 0, 1),
+    ("turn_weight", 0, 0, 1),
+    ("copy_weight", 0, 0, 1, False),
+    ("turn_weight", 0, 0, 0),
+    ("quantize_u", 0),
+    ("copy_weight", 0, 0, 0, False),
+    ("times_amp", 1, 0),
+    ("load_weight", 0, 2),
+    ("turn_weight", 0, 1, 0),
+    ("load_weight", 1, 0),
+    ("turn_weight", 0, 1, 1),
+    ("turn_weight", 0, 2, 1),
+    ("quantize_weight", 0, 0),
+    ("copy_weight", 0, 1, 0, False),
+    ("turn_weight", 0, 2, 0),
+    ("load_u", 1),
+    ("copy_weight", 0, 1, 1, True),
+    ("sine", 1, 1),
+    ("copy_weight", 0, 2, 1, False),
+    ("load_weight", 1, 1),
+    ("load_weight", 1, 2),
+    ("load_phases", 2, 1),
+    ("copy_weight", 0, 2, 0, False),
+    ("turn_weight", 1, 0, 1),
+    ("turn_weight", 1, 0, 0),
+    ("turn_weight", 1, 1, 0),
+    ("turn_weight", 1, 1, 1),
+    ("turn_weight", 1, 2, 1),
+    ("turn_weight", 1, 2, 0),
+    ("quantize_psi", 1, 0),
+    ("quantize_weight", 0, 1),
+    ("times_amp", 1, 1),
+    ("load_unit",),
+    ("quantize_weight", 0, 2),
+    ("multiply", 0, 0, 0),
+    ("quantize_psi", 1, 1),
+    ("copy_weight", 1, 1, 0, True),
+    ("load_phases", 2, 0),
+    ("load_phases", 4, 1),
+    ("copy_weight", 1, 0, 1, False),
+    ("interleave_u", 1, True),
+    ("copy_weight", 1, 0, 0, False),
+    ("load_phases", 3, 1),
+    ("multiply", 0, 0, 3),
+    ("quantize_u", 1),
+    ("copy_weight", 1, 1, 1, False),
+    ("quantize_weight", 1, 0),
+    ("affine",),
+    ("sine", 2, 1),
+    ("copy_weight", 1, 2, 1, True),
+    ("finish", 0, 0, 0, False),
+    ("load_u", 2),
+    ("quantize_weight", 1, 1),
+    ("multiply", 0, 0, 1),
+    ("finish", 0, 0, 1, False),
+    ("multiply", 0, 0, 2),
+    ("copy_weight", 1, 2, 0, True),
+    ("finish", 0, 0, 3, True),
+    ("finish", 0, 0, 2, False),
+    ("sine", 2, 0),
+    ("load_phases", 4, 0),
+    ("load_phases", 3, 0),
+    ("multiply", 1, 0, 0),
+    ("quantize_weight", 1, 2),
+    ("multiply", 0, 1, 2),
+    ("multiply", 0, 1, 1),
+    ("multiply", 0, 1, 0),
+    ("finish", 0, 1, 1, False),
+    ("multiply", 0, 1, 3),
+    ("multiply", 1, 0, 3),
+    ("times_amp", 2, 1),
+    ("interleave_u", 2, True),
+    ("finish", 0, 1, 0, False),
+    ("finish", 0, 1, 2, True),
+    ("quantize_psi", 2, 1),
+    ("multiply", 1, 1, 2),
+    ("sine", 3, 1),
+    ("multiply", 1, 0, 2),
+    ("finish", 1, 0, 0, False),
+    ("finish", 1, 1, 2, False),
+    ("finish", 1, 0, 2, False),
+    ("finish", 0, 1, 3, True),
+    ("times_amp", 2, 0),
+    ("quantize_u", 2),
+    ("quantize_psi", 2, 0),
+    ("multiply", 1, 0, 1),
+    ("multiply", 1, 1, 0),
+    ("interleave_y", 0, 0),
+    ("multiply", 1, 1, 1),
+    ("load_u", 3),
+    ("finish", 1, 0, 3, False),
+    ("multiply", 2, 0, 0),
+    ("finish", 1, 1, 1, False),
+    ("store_y", 0, 0),
+    ("sine", 3, 0),
+    ("finish", 1, 0, 1, True),
+    ("interleave_y", 0, 1),
+    ("quantize_y", 0, 0),
+    ("multiply", 2, 0, 2),
+    ("quantize_y", 0, 1),
+    ("multiply", 1, 1, 3),
+    ("times_amp", 3, 1),
+    ("multiply", 2, 0, 3),
+    ("interleave_y", 1, 0),
+    ("finish", 1, 1, 0, False),
+    ("store_y", 0, 1),
+    ("store_y", 1, 0),
+    ("store_words", 0, 0),
+    ("load_u", 4),
+    ("multiply", 2, 0, 1),
+    ("multiply", 2, 1, 0),
+    ("finish", 1, 1, 3, True),
+    ("finish", 2, 0, 2, False),
+    ("multiply", 2, 1, 3),
+    ("finish", 2, 0, 1, False),
+    ("finish", 2, 0, 0, False),
+    ("multiply", 2, 1, 2),
+    ("quantize_y", 1, 0),
+    ("store_words", 0, 1),
+    ("times_amp", 3, 0),
+    ("finish", 2, 0, 3, False),
+    ("multiply", 2, 1, 1),
+    ("quantize_psi", 3, 1),
+    ("interleave_y", 1, 1),
+    ("store_y", 1, 1),
+    ("interleave_u", 3, True),
+    ("quantize_psi", 3, 0),
+    ("store_y", 2, 0),
+    ("quantize_u", 3),
+    ("finish", 2, 1, 3, False),
+    ("finish", 2, 1, 0, False),
+    ("finish", 2, 1, 2, True),
+    ("store_words", 1, 0),
+    ("multiply", 3, 0, 3),
+    ("interleave_y", 2, 0),
+    ("multiply", 3, 0, 1),
+    ("quantize_y", 1, 1),
+    ("finish", 2, 1, 1, False),
+    ("quantize_y", 2, 0),
+    ("multiply", 3, 0, 2),
+    ("interleave_y", 2, 1),
+    ("sine", 4, 0),
+    ("finish", 3, 0, 1, False),
+    ("times_amp", 4, 0),
+    ("finish", 3, 0, 3, False),
+    ("finish", 3, 0, 2, False),
+    ("multiply", 3, 0, 0),
+    ("multiply", 3, 1, 2),
+    ("multiply", 3, 1, 1),
+    ("quantize_y", 2, 1),
+    ("store_y", 2, 1),
+    ("finish", 3, 0, 0, False),
+    ("sine", 4, 1),
+    ("store_words", 1, 1),
+    ("multiply", 3, 1, 3),
+    ("quantize_psi", 4, 0),
+    ("finish", 3, 1, 1, True),
+    ("times_amp", 4, 1),
+    ("interleave_u", 4, True),
+    ("finish", 3, 1, 3, False),
+    ("store_words", 2, 0),
+    ("finish", 3, 1, 2, False),
+    ("quantize_u", 4),
+    ("quantize_psi", 4, 1),
+    ("multiply", 3, 1, 0),
+    ("interleave_y", 3, 0),
+    ("multiply", 4, 1, 3),
+    ("finish", 3, 1, 0, False),
+    ("multiply", 4, 1, 1),
+    ("quantize_y", 3, 0),
+    ("interleave_y", 3, 1),
+    ("store_y", 3, 0),
+    ("multiply", 4, 1, 2),
+    ("store_words", 2, 1),
+    ("multiply", 4, 0, 1),
+    ("quantize_y", 3, 1),
+    ("multiply", 4, 1, 0),
+    ("finish", 4, 1, 3, False),
+    ("finish", 4, 1, 1, False),
+    ("store_y", 3, 1),
+    ("multiply", 4, 0, 0),
+    ("finish", 4, 1, 2, False),
+    ("multiply", 4, 0, 3),
+    ("finish", 4, 1, 0, False),
+    ("multiply", 4, 0, 2),
+    ("finish", 4, 0, 1, True),
+    ("finish", 4, 0, 0, False),
+    ("finish", 4, 0, 3, False),
+    ("interleave_y", 4, 1),
+    ("finish", 4, 0, 2, False),
+    ("store_words", 3, 0),
+    ("store_y", 4, 1),
+    ("interleave_y", 4, 0),
+    ("quantize_y", 4, 1),
+    ("store_words", 3, 1),
+    ("early_scales",),
+    ("store_y", 4, 0),
+    ("quantize_y", 4, 0),
+    ("store_words", 4, 0),
+    ("store_words", 4, 1),
+    ("late_scales",),
+]
+
+
+def tile_koopman_control_step_g2_kernel(tc, phases, amp, koopman, control, u, drift, unit, out_0, out_1, out_2):
+    nc = tc.nc
+    with ExitStack() as ctx:
+        keep = ctx.enter_context(tc.tile_pool(name="keep", bufs=1))
+        psum = ctx.enter_context(tc.psum_pool(name="psum", bufs=1))
+        ctx.enter_context(tc.manual_schedule())
+
+        def ring(name, count, shape, dtype):
+            return [keep.tile(shape, dtype, name="%s%d" % (name, j), align_bytes=64) for j in range(count)]
+
+        banks = [psum.tile([P, BANK], F32, name="bank%d" % j) for j in range(BANKS)]
+        ident = keep.tile([P, P], F32, name="ident")
+        zero = keep.tile([P, 1], F32, name="zero")
+        zero_bias = keep.tile([P, 1], F32, name="zero_bias")
+        amp_sb = keep.tile([P, GROUPS, PACK], BF16, name="amp_sb")
+        drift_sb = keep.tile([P, GROUPS, PACK], BF16, name="drift_sb")
+        unit_sb = keep.tile([P, GROUPS, PACK], BF16, name="unit_sb")
+        unit32 = keep.tile([P, GROUPS, PACK], F32, name="unit32")
+        bias32 = keep.tile([P, GROUPS, PACK], F32, name="bias32")
+
+        ph_raw = [[keep.tile([P, PACK, w], BF16, name="ph%d_%d" % (n, c)) for c in range(PSI_PASSES)] for n, w in enumerate(WIDTHS)]
+        u_raw = [keep.tile([P, PACK, w], BF16, name="u%d" % n) for n, w in enumerate(WIDTHS)]
+        w_raw = [ring("w_raw%d_" % g, PASSES, [P, PACK, K_PASS], BF16) for g in range(GROUPS)]
+        sin32 = ring("sin", SIN_BUFS, [P, PACK, BANK], F32)
+        psi_bf = ring("psi_bf", PSI_BUFS, [P, PACK * BANK], BF16)
+        u_bf = ring("u_bf", U_BUFS, [P, PACK * BANK], BF16)
+        w_bf = ring("w_bf", W_BUFS, [P, PACK * K_PASS], BF16)
+        y32 = ring("y32_", Y_BUFS, [P, PACK, BANK], F32)
+        y_bf = ring("y_bf", YB_BUFS, [P, PACK * BANK], BF16)
+        x_codes = [[keep.tile([P, w], U32, name="xc%d_%d" % (n, c), align_bytes=64) for c in range(PASSES)] for n, w in enumerate(WIDTHS)]
+        x_scales = [[keep.tile([P, w], U8, name="xs%d_%d" % (n, c), align_bytes=64) for c in range(PASSES)] for n, w in enumerate(WIDTHS)]
+        w_codes = [ring("wc%d_" % g, PASSES, [P, K_PASS], U32) for g in range(GROUPS)]
+        w_scales = [ring("ws%d_" % g, PASSES, [P, K_PASS], U8) for g in range(GROUPS)]
+        y_codes = [[keep.tile([P, w], U32, name="yc%d_%d" % (n, g), align_bytes=64) for g in range(GROUPS)] for n, w in enumerate(WIDTHS)]
+        early_width = STARTS[EARLY_CHUNKS]
+        y_scales_early = keep.tile([P, GROUPS, early_width], U8, name="ys_early", align_bytes=64)
+        y_scales_late = keep.tile([P, GROUPS, T - early_width], U8, name="ys_late", align_bytes=64)
+
+        words_out = out_1.rearrange("g p m t -> g p (m t)").bitcast(I32)
+        scales_out = out_2.bitcast(I32)
+
+        def cols(n):
+            return slice(STARTS[n], STARTS[n] + WIDTHS[n])
+
+        def rows(c):
+            return slice(c * K_PASS, (c + 1) * K_PASS)
+
+        def load_vector(dst, src):
+            nc.sync.dma_start(out=dst[:], in_=src.rearrange("(g p t) -> p g t", p=P, t=PACK))
+
+        def load_phases(n, c):
+            nc.sync.dma_start(out=ph_raw[n][c][:], in_=phases[rows(c), cols(n)].rearrange("(p t) m -> p t m", t=PACK))
+
+        def load_u(n):
+            nc.sync.dma_start(out=u_raw[n][:], in_=u[:, cols(n)].rearrange("(p t) m -> p t m", t=PACK))
+
+        def load_weight(g, c):
+            src = control[rows(g), :] if c == U_PASS else koopman[rows(g), rows(c)]
+            nc.sync.dma_start(out=w_raw[g][c][:], in_=src.rearrange("(p t) k -> p t k", t=PACK))
+
+        def interleaved(tile_bf, w, run):
+            return tile_bf[:, : PACK * w].rearrange("p (b i t) -> p b t i", i=run, t=PACK)
+
+        def by_slot(tile, w, run):
+            return tile[:, :, :w].rearrange("p t (b i) -> p b t i", i=run)
+
+        def quantize(codes, scales, src):
+            nc.vector.quantize_mx(out=codes.bitcast(FP8X4), scales=scales, in_=src)
+
+        def sine(n, c):
+            j = PSI_PASSES * n + c
+            nc.scalar.activation(out=sin32[j % SIN_BUFS][:, :, : WIDTHS[n]], in_=ph_raw[n][c][:], func=ACT.Sin, bias=zero_bias[:])
+
+        def times_amp(n, c):
+            j, w = PSI_PASSES * n + c, WIDTHS[n]
+            factor = amp_sb[:, c, :].unsqueeze(1).unsqueeze(3).to_broadcast([P, w // 2, PACK, 2])
+            nc.vector.tensor_tensor(out=interleaved(psi_bf[j % PSI_BUFS], w, 2), in0=by_slot(sin32[j % SIN_BUFS], w, 2), in1=factor, op=ALU.mult)
+
+        def quantize_psi(n, c):
+            j = PSI_PASSES * n + c
+            quantize(x_codes[n][c][:], x_scales[n][c][:], psi_bf[j % PSI_BUFS][:, : PACK * WIDTHS[n]])
+
+        def interleave_u(n, on_scalar=False):
+            dst, src = interleaved(u_bf[n % U_BUFS], WIDTHS[n], 4), by_slot(u_raw[n], WIDTHS[n], 4)
+            if on_scalar:
+                nc.scalar.copy(out=dst, in_=src)
+            else:
+                nc.vector.tensor_copy(out=dst, in_=src)
+
+        def quantize_u(n):
+            quantize(x_codes[n][U_PASS][:], x_scales[n][U_PASS][:], u_bf[n % U_BUFS][:, : PACK * WIDTHS[n]])
+
+        W_BANKS = GROUPS * PASSES * 2
+
+        def turn_weight(g, c, half):
+            bank = banks[((g * PASSES + c) * 2 + half) % BANKS]
+            for s in range(2):
+                words = w_raw[g][c][:, 2 * half + s, :].bitcast(F32)
+                for e in range(2):
+                    at = (2 * s + e) * P
+                    nc.tensor.transpose(bank[:, at : at + P], words[:, e : K_PASS // 2 : 2], ident[:])
+
+        def copy_weight(g, c, half, on_vector=False):
+            bank = banks[((g * PASSES + c) * 2 + half) % BANKS]
+            dst = w_bf[(g * PASSES + c) % W_BUFS][:].bitcast(F32)[:, half * BANK : (half + 1) * BANK]
+            dst, src = dst.rearrange("p (s m e) -> p s m e", s=2, e=2), bank[:].rearrange("p (s e m) -> p s m e", s=2, e=2)
+            if on_vector:
+                nc.vector.tensor_copy(out=dst, in_=src)
+            else:
+                nc.scalar.copy(out=dst, in_=src)
+
+        def quantize_weight(g, c):
+            quantize(w_codes[g][c][:], w_scales[g][c][:], w_bf[(g * PASSES + c) % W_BUFS][:])
+
+        def acc_bank(n, g, t):
+            return banks[(W_BANKS + (GROUPS * n + g) * PACK + t) % BANKS][:, : WIDTHS[n]]
+
+        def multiply(n, g, t):
+            m = slice(t * P, (t + 1) * P)
+            for c in range(PASSES):
+                nc.tensor.matmul_mx(
+                    out=acc_bank(n, g, t),
+                    lhsT=w_codes[g][c][:, m].bitcast(FP8X4),
+                    lhsT_scale=w_scales[g][c][:, m],
+                    rhs=x_codes[n][c][:].bitcast(FP8X4),
+                    rhs_scale=x_scales[n][c][:],
+                    start=(c == 0),
+                    stop=(c == PASSES - 1),
+                )
+
+        def y_tile(n, g):
+            return y32[(GROUPS * n + g) % Y_BUFS]
+
+        def finish(n, g, t, on_vector=False):
+            dst = y_tile(n, g)[:, t, : WIDTHS[n]]
+            scale, bias = unit32[:, g, t : t + 1], bias32[:, g, t : t + 1]
+            if on_vector:
+                nc.vector.tensor_scalar(out=dst, in0=acc_bank(n, g, t), scalar1=scale, scalar2=bias, op0=ALU.mult, op1=ALU.add)
+            else:
+                nc.scalar.activation(out=dst, in_=acc_bank(n, g, t), func=ACT.Identity, bias=bias, scale=scale)
+
+        def store_y(n, g):
+            nc.sync.dma_start(out=out_0[rows(g), cols(n)].rearrange("(p t) m -> p t m", t=PACK), in_=y_tile(n, g)[:, :, : WIDTHS[n]])
+
+        def interleave_y(n, g):
+            w = WIDTHS[n]
+            nc.vector.tensor_copy(out=interleaved(y_bf[(GROUPS * n + g) % YB_BUFS], w, 2), in_=by_slot(y_tile(n, g), w, 2))
+
+        def quantize_y(n, g):
+            if n < EARLY_CHUNKS:
+                scales = y_scales_early[:, g, cols(n)]
+            else:
+                scales = y_scales_late[:, g, STARTS[n] - early_width : STARTS[n] - early_width + WIDTHS[n]]
+            quantize(y_codes[n][g][:], scales, y_bf[(GROUPS * n + g) % YB_BUFS][:, : PACK * WIDTHS[n]])
+
+        def store_words(n, g):
+            nc.sync.dma_start(out=words_out[g, :, cols(n)], in_=y_codes[n][g][:].bitcast(I32))
+
+        def store_scales(tile, first, last):
+            for q in range(4):
+                nc.sync.dma_start(
+                    out=scales_out[:, 4 * q : 4 * q + 4, first // 4 : last // 4].rearrange("g r m -> r g m"),
+                    in_=tile[32 * q : 32 * q + 4, :, :].bitcast(I32),
+                )
+
+        def prepare():
+            nc.vector.memset(zero[:], 0.0)
+            nc.scalar.activation(out=zero_bias[:], in_=zero[:], func=ACT.Sin)
+            make_identity(nc, ident[:])
+
+        def load_amp():
+            load_vector(amp_sb, amp)
+
+        def load_unit():
+            load_vector(unit_sb, unit)
+            load_vector(drift_sb, drift)
+
+        def affine():
+            nc.vector.tensor_copy(out=unit32[:], in_=unit_sb[:])
+            nc.vector.tensor_tensor(out=bias32[:], in0=drift_sb[:], in1=unit_sb[:], op=ALU.mult)
+
+        def early_scales():
+            store_scales(y_scales_early, 0, early_width)
+
+        def late_scales():
+            store_scales(y_scales_late, early_width, T)
+
+        steps = dict(
+            prepare=prepare, load_amp=load_amp, load_unit=load_unit, affine=affine, early_scales=early_scales, late_scales=late_scales,
+            load_phases=load_phases, load_u=load_u, load_weight=load_weight, sine=sine, times_amp=times_amp, quantize_psi=quantize_psi,
+            interleave_u=interleave_u, quantize_u=quantize_u, turn_weight=turn_weight, copy_weight=copy_weight,
+            quantize_weight=quantize_weight, multiply=multiply, finish=finish, store_y=store_y, interleave_y=interleave_y,
+            quantize_y=quantize_y, store_words=store_words,
+        )
+        for name, *args in ORDER:
+            steps[name](*args)

@@ -28,226 +28,262 @@ WIDTHS = [256, 512, 512, 512, 256]
 STARTS = [sum(WIDTHS[:n]) for n in range(len(WIDTHS))]
 CHUNKS = len(WIDTHS)
 EARLY_CHUNKS = CHUNKS - 1
-SIN_BUFS, PSI_BUFS, U_BUFS, W_BUFS, Y_BUFS, YB_BUFS = 2, 2, 1, 2, 5, 2
+SCALE_STORES = [[0, 1], [2, 3], [4]]
+LOADS = [[0], [1], [2, 3, 4]]
+STORES = [[0], [1], [2], [3], [4]]
+WORD_STORES = STORES
+STORE_SLOTS = 2
+UNITS = [(0,0),(1,0),(0,1),(1,1),(2,0),(2,1),(3,0),(3,1),(4,0),(4,1)]
+SIN_BUFS, PSI_BUFS, U_BUFS, YB_BUFS, X_BUFS, W_BUFS = 3, 3, 2, 3, 3, 2
+
+
+def span(chunks):
+    return slice(STARTS[chunks[0]], STARTS[chunks[-1]] + WIDTHS[chunks[-1]])
+
+
+def place(groups, n):
+    for j, chunks in enumerate(groups):
+        if n in chunks:
+            first = STARTS[n] - STARTS[chunks[0]]
+            return j, slice(first, first + WIDTHS[n])
+
+
+def width(chunks):
+    return sum(WIDTHS[n] for n in chunks)
+
 
 ORDER = [
     ("load_phases", 0, 0),
     ("prepare",),
-    ("sine", 0, 0),
     ("load_amp",),
-    ("times_amp", 0, 0),
     ("load_phases", 0, 1),
-    ("sine", 0, 1),
     ("load_phases", 1, 0),
-    ("load_weight", 0, 0),
-    ("times_amp", 0, 1),
-    ("load_u", 0),
-    ("load_weight", 0, 1),
+    ("load_koopman", 0, 1),
+    ("load_koopman", 0, 0),
     ("load_phases", 1, 1),
-    ("sine", 1, 0),
-    ("quantize_psi", 0, 0),
-    ("interleave_u", 0, False),
-    ("quantize_psi", 0, 1),
-    ("turn_weight", 0, 0, 1),
-    ("copy_weight", 0, 0, 1, False),
-    ("turn_weight", 0, 0, 0),
-    ("quantize_u", 0),
-    ("copy_weight", 0, 0, 0, False),
-    ("times_amp", 1, 0),
-    ("load_weight", 0, 2),
-    ("turn_weight", 0, 1, 0),
-    ("load_weight", 1, 0),
-    ("turn_weight", 0, 1, 1),
-    ("turn_weight", 0, 2, 1),
-    ("quantize_weight", 0, 0),
-    ("copy_weight", 0, 1, 0, False),
-    ("turn_weight", 0, 2, 0),
+    ("load_control", 0),
+    ("load_koopman", 1, 0),
+    ("load_koopman", 1, 1),
+    ("sine", 0, 0),
+    ("load_u", 0),
+    ("sine", 0, 1),
+    ("times_amp", 0, 0),
     ("load_u", 1),
-    ("copy_weight", 0, 1, 1, True),
-    ("sine", 1, 1),
-    ("copy_weight", 0, 2, 1, False),
-    ("load_weight", 1, 1),
-    ("load_weight", 1, 2),
-    ("load_phases", 2, 1),
-    ("copy_weight", 0, 2, 0, False),
-    ("turn_weight", 1, 0, 1),
-    ("turn_weight", 1, 0, 0),
-    ("turn_weight", 1, 1, 0),
-    ("turn_weight", 1, 1, 1),
-    ("turn_weight", 1, 2, 1),
-    ("turn_weight", 1, 2, 0),
-    ("quantize_psi", 1, 0),
-    ("quantize_weight", 0, 1),
-    ("times_amp", 1, 1),
-    ("load_unit",),
-    ("quantize_weight", 0, 2),
-    ("multiply", 0, 0, 0),
-    ("quantize_psi", 1, 1),
-    ("copy_weight", 1, 1, 0, True),
+    ("sine", 1, 0),
+    ("times_amp", 0, 1),
+    ("load_control", 1),
+    ("turn_weight", 0, 0, 1),
+    ("quantize_psi", 0, 1),
+    ("quantize_psi", 0, 0),
     ("load_phases", 2, 0),
-    ("load_phases", 4, 1),
-    ("copy_weight", 1, 0, 1, False),
-    ("interleave_u", 1, True),
-    ("copy_weight", 1, 0, 0, False),
-    ("load_phases", 3, 1),
-    ("multiply", 0, 0, 3),
-    ("quantize_u", 1),
-    ("copy_weight", 1, 1, 1, False),
-    ("quantize_weight", 1, 0),
-    ("affine",),
-    ("sine", 2, 1),
-    ("copy_weight", 1, 2, 1, True),
-    ("finish", 0, 0, 0, False),
+    ("turn_weight", 0, 0, 0),
+    ("times_amp", 1, 0),
+    ("copy_weight", 0, 0, 1, False),
+    ("turn_weight", 0, 1, 0),
+    ("load_unit",),
+    ("copy_weight", 0, 0, 0, False),
+    ("sine", 1, 1),
+    ("turn_weight", 0, 1, 1),
+    ("quantize_weight", 0, 0),
+    ("quantize_psi", 1, 0),
+    ("turn_weight", 0, 2, 0),
+    ("load_phases", 2, 1),
+    ("copy_weight", 0, 1, 0, False),
+    ("turn_weight", 0, 2, 1),
+    ("times_amp", 1, 1),
+    ("copy_weight", 0, 2, 0, False),
     ("load_u", 2),
-    ("quantize_weight", 1, 1),
-    ("multiply", 0, 0, 1),
-    ("finish", 0, 0, 1, False),
+    ("turn_weight", 1, 0, 0),
+    ("copy_weight", 0, 2, 1, False),
+    ("copy_weight", 0, 1, 1, False),
+    ("turn_weight", 1, 0, 1),
+    ("interleave_u", 0, 1),
+    ("quantize_weight", 0, 1),
+    ("turn_weight", 1, 1, 1),
+    ("quantize_weight", 0, 2),
+    ("copy_weight", 1, 0, 0, False),
+    ("interleave_u", 1, 0),
+    ("turn_weight", 1, 1, 0),
+    ("copy_weight", 1, 0, 1, False),
+    ("copy_weight", 1, 1, 1, False),
+    ("turn_weight", 1, 2, 0),
+    ("quantize_weight", 1, 0),
+    ("copy_weight", 1, 1, 0, False),
+    ("quantize_u", 0),
+    ("quantize_u", 1),
+    ("turn_weight", 1, 2, 1),
+    ("copy_weight", 1, 2, 0, False),
+    ("quantize_psi", 1, 1),
     ("multiply", 0, 0, 2),
-    ("copy_weight", 1, 2, 0, True),
-    ("finish", 0, 0, 3, True),
-    ("finish", 0, 0, 2, False),
     ("sine", 2, 0),
-    ("load_phases", 4, 0),
-    ("load_phases", 3, 0),
-    ("multiply", 1, 0, 0),
+    ("affine",),
+    ("multiply", 0, 0, 0),
+    ("copy_weight", 1, 2, 1, True),
+    ("multiply", 0, 0, 1),
+    ("quantize_weight", 1, 1),
+    ("multiply", 0, 0, 3),
     ("quantize_weight", 1, 2),
-    ("multiply", 0, 1, 2),
-    ("multiply", 0, 1, 1),
-    ("multiply", 0, 1, 0),
-    ("finish", 0, 1, 1, False),
-    ("multiply", 0, 1, 3),
-    ("multiply", 1, 0, 3),
-    ("times_amp", 2, 1),
-    ("interleave_u", 2, True),
-    ("finish", 0, 1, 0, False),
-    ("finish", 0, 1, 2, True),
-    ("quantize_psi", 2, 1),
-    ("multiply", 1, 1, 2),
-    ("sine", 3, 1),
-    ("multiply", 1, 0, 2),
-    ("finish", 1, 0, 0, False),
-    ("finish", 1, 1, 2, False),
-    ("finish", 1, 0, 2, False),
-    ("finish", 0, 1, 3, True),
-    ("times_amp", 2, 0),
-    ("quantize_u", 2),
-    ("quantize_psi", 2, 0),
     ("multiply", 1, 0, 1),
-    ("multiply", 1, 1, 0),
-    ("interleave_y", 0, 0),
-    ("multiply", 1, 1, 1),
-    ("load_u", 3),
-    ("finish", 1, 0, 3, False),
-    ("multiply", 2, 0, 0),
-    ("finish", 1, 1, 1, False),
-    ("store_y", 0, 0),
-    ("sine", 3, 0),
-    ("finish", 1, 0, 1, True),
-    ("interleave_y", 0, 1),
+    ("finish", 0, 0, 1, True),
+    ("finish", 0, 0, 2, False),
+    ("finish", 0, 0, 0, False),
+    ("times_amp", 2, 0),
+    ("multiply", 1, 0, 2),
+    ("finish", 0, 0, 3, False),
+    ("finish", 1, 0, 1, False),
+    ("store_y", 0, 0, 0, 0),
+    ("multiply", 0, 1, 1),
+    ("store_y", 0, 0, 1, 0),
+    ("sine", 2, 1),
+    ("multiply", 0, 1, 0),
+    ("multiply", 0, 1, 3),
+    ("multiply", 1, 0, 0),
+    ("interleave_y", 0, 0, 0),
+    ("finish", 0, 1, 1, True),
+    ("multiply", 0, 1, 2),
     ("quantize_y", 0, 0),
-    ("multiply", 2, 0, 2),
-    ("quantize_y", 0, 1),
+    ("finish", 0, 1, 0, False),
+    ("quantize_psi", 2, 0),
+    ("multiply", 1, 0, 3),
+    ("finish", 1, 0, 0, False),
+    ("store_words", 0, 0, 0),
+    ("store_y", 0, 1, 0, 0),
+    ("times_amp", 2, 1),
+    ("finish", 1, 0, 2, False),
+    ("multiply", 1, 1, 0),
+    ("store_y", 1, 0, 0, 0),
+    ("finish", 1, 0, 3, False),
+    ("finish", 0, 1, 3, False),
+    ("multiply", 1, 1, 2),
+    ("finish", 0, 1, 2, False),
+    ("store_y", 1, 0, 1, 0),
+    ("sine", 3, 0),
+    ("interleave_u", 2, 0),
     ("multiply", 1, 1, 3),
-    ("times_amp", 3, 1),
-    ("multiply", 2, 0, 3),
-    ("interleave_y", 1, 0),
-    ("finish", 1, 1, 0, False),
-    ("store_y", 0, 1),
-    ("store_y", 1, 0),
-    ("store_words", 0, 0),
-    ("load_u", 4),
+    ("store_y", 0, 1, 1, 0),
+    ("multiply", 1, 1, 1),
+    ("quantize_psi", 2, 1),
+    ("quantize_u", 2),
     ("multiply", 2, 0, 1),
-    ("multiply", 2, 1, 0),
-    ("finish", 1, 1, 3, True),
-    ("finish", 2, 0, 2, False),
+    ("finish", 1, 1, 3, False),
+    ("interleave_u", 3, 0),
+    ("finish", 1, 1, 2, False),
     ("multiply", 2, 1, 3),
-    ("finish", 2, 0, 1, False),
-    ("finish", 2, 0, 0, False),
-    ("multiply", 2, 1, 2),
-    ("quantize_y", 1, 0),
-    ("store_words", 0, 1),
+    ("finish", 1, 1, 0, False),
+    ("store_y", 1, 1, 1, 0),
+    ("finish", 1, 1, 1, False),
     ("times_amp", 3, 0),
-    ("finish", 2, 0, 3, False),
-    ("multiply", 2, 1, 1),
-    ("quantize_psi", 3, 1),
-    ("interleave_y", 1, 1),
-    ("store_y", 1, 1),
-    ("interleave_u", 3, True),
-    ("quantize_psi", 3, 0),
-    ("store_y", 2, 0),
+    ("multiply", 2, 1, 2),
+    ("sine", 3, 1),
+    ("store_y", 1, 1, 0, 0),
+    ("multiply", 2, 0, 0),
+    ("multiply", 2, 1, 0),
     ("quantize_u", 3),
     ("finish", 2, 1, 3, False),
-    ("finish", 2, 1, 0, False),
-    ("finish", 2, 1, 2, True),
-    ("store_words", 1, 0),
-    ("multiply", 3, 0, 3),
-    ("interleave_y", 2, 0),
-    ("multiply", 3, 0, 1),
-    ("quantize_y", 1, 1),
+    ("multiply", 2, 1, 1),
+    ("times_amp", 3, 1),
+    ("finish", 2, 1, 2, False),
+    ("multiply", 2, 0, 2),
+    ("finish", 2, 0, 0, False),
+    ("store_y", 2, 1, 1, 0),
+    ("finish", 2, 0, 1, False),
+    ("multiply", 2, 0, 3),
     ("finish", 2, 1, 1, False),
-    ("quantize_y", 2, 0),
-    ("multiply", 3, 0, 2),
-    ("interleave_y", 2, 1),
-    ("sine", 4, 0),
-    ("finish", 3, 0, 1, False),
-    ("times_amp", 4, 0),
-    ("finish", 3, 0, 3, False),
-    ("finish", 3, 0, 2, False),
-    ("multiply", 3, 0, 0),
+    ("quantize_psi", 3, 0),
+    ("store_y", 2, 0, 0, 0),
+    ("finish", 2, 1, 0, False),
+    ("quantize_psi", 3, 1),
     ("multiply", 3, 1, 2),
-    ("multiply", 3, 1, 1),
-    ("quantize_y", 2, 1),
-    ("store_y", 2, 1),
-    ("finish", 3, 0, 0, False),
-    ("sine", 4, 1),
-    ("store_words", 1, 1),
+    ("finish", 2, 0, 2, False),
+    ("interleave_y", 1, 0, 0),
+    ("store_y", 2, 1, 0, 0),
+    ("finish", 2, 0, 3, False),
     ("multiply", 3, 1, 3),
-    ("quantize_psi", 4, 0),
-    ("finish", 3, 1, 1, True),
-    ("times_amp", 4, 1),
-    ("interleave_u", 4, True),
-    ("finish", 3, 1, 3, False),
-    ("store_words", 2, 0),
+    ("sine", 4, 1),
+    ("store_y", 2, 0, 1, 0),
+    ("interleave_y", 0, 1, 0),
+    ("multiply", 3, 0, 3),
+    ("quantize_y", 1, 0),
     ("finish", 3, 1, 2, False),
-    ("quantize_u", 4),
-    ("quantize_psi", 4, 1),
+    ("interleave_y", 1, 1, 0),
+    ("finish", 3, 1, 3, False),
+    ("multiply", 3, 0, 2),
+    ("store_words", 1, 0, 0),
+    ("sine", 4, 0),
+    ("store_y", 3, 1, 1, 0),
+    ("multiply", 3, 1, 1),
+    ("quantize_y", 0, 1),
+    ("quantize_y", 1, 1),
+    ("finish", 3, 0, 3, False),
     ("multiply", 3, 1, 0),
-    ("interleave_y", 3, 0),
-    ("multiply", 4, 1, 3),
+    ("store_words", 0, 1, 0),
+    ("times_amp", 4, 1),
+    ("finish", 3, 0, 2, False),
+    ("store_words", 1, 1, 0),
+    ("store_scales", 0, 0, 0),
+    ("store_scales", 0, 1, 0),
+    ("multiply", 3, 0, 0),
+    ("store_scales", 0, 2, 0),
+    ("interleave_u", 4, 1),
+    ("store_scales", 0, 3, 0),
+    ("store_y", 3, 0, 1, 0),
+    ("times_amp", 4, 0),
+    ("multiply", 3, 0, 1),
+    ("finish", 3, 1, 1, False),
+    ("quantize_psi", 4, 1),
     ("finish", 3, 1, 0, False),
-    ("multiply", 4, 1, 1),
-    ("quantize_y", 3, 0),
-    ("interleave_y", 3, 1),
-    ("store_y", 3, 0),
-    ("multiply", 4, 1, 2),
-    ("store_words", 2, 1),
-    ("multiply", 4, 0, 1),
-    ("quantize_y", 3, 1),
-    ("multiply", 4, 1, 0),
-    ("finish", 4, 1, 3, False),
-    ("finish", 4, 1, 1, False),
-    ("store_y", 3, 1),
-    ("multiply", 4, 0, 0),
-    ("finish", 4, 1, 2, False),
+    ("quantize_psi", 4, 0),
+    ("quantize_u", 4),
+    ("finish", 3, 0, 0, False),
+    ("interleave_y", 2, 0, 0),
     ("multiply", 4, 0, 3),
-    ("finish", 4, 1, 0, False),
+    ("store_y", 3, 1, 0, 0),
+    ("multiply", 4, 1, 3),
+    ("finish", 3, 0, 1, False),
     ("multiply", 4, 0, 2),
-    ("finish", 4, 0, 1, True),
-    ("finish", 4, 0, 0, False),
     ("finish", 4, 0, 3, False),
-    ("interleave_y", 4, 1),
+    ("interleave_y", 2, 1, 0),
+    ("multiply", 4, 0, 0),
+    ("finish", 4, 1, 3, False),
+    ("store_y", 3, 0, 0, 0),
     ("finish", 4, 0, 2, False),
-    ("store_words", 3, 0),
-    ("store_y", 4, 1),
-    ("interleave_y", 4, 0),
-    ("quantize_y", 4, 1),
-    ("store_words", 3, 1),
-    ("early_scales",),
-    ("store_y", 4, 0),
+    ("multiply", 4, 1, 1),
+    ("finish", 4, 0, 0, False),
+    ("multiply", 4, 1, 2),
+    ("store_y", 4, 0, 1, 0),
+    ("interleave_y", 3, 0, 1),
+    ("quantize_y", 2, 0),
+    ("multiply", 4, 0, 1),
+    ("multiply", 4, 1, 0),
+    ("finish", 4, 1, 2, True),
+    ("quantize_y", 2, 1),
+    ("store_words", 2, 0, 0),
+    ("store_y", 4, 1, 1, 0),
+    ("interleave_y", 3, 1, 0),
+    ("store_words", 2, 1, 0),
+    ("finish", 4, 0, 1, False),
+    ("interleave_y", 4, 0, 1),
+    ("quantize_y", 3, 0),
+    ("store_y", 4, 0, 0, 0),
+    ("quantize_y", 3, 1),
+    ("store_words", 3, 0, 0),
+    ("finish", 4, 1, 1, False),
+    ("finish", 4, 1, 0, False),
     ("quantize_y", 4, 0),
-    ("store_words", 4, 0),
-    ("store_words", 4, 1),
-    ("late_scales",),
+    ("store_words", 3, 1, 0),
+    ("store_scales", 1, 0, 0),
+    ("store_scales", 1, 1, 0),
+    ("store_scales", 1, 2, 0),
+    ("store_scales", 1, 3, 0),
+    ("interleave_y", 4, 1, 0),
+    ("store_y", 4, 1, 0, 0),
+    ("quantize_y", 4, 1),
+    ("store_words", 4, 0, 0),
+    ("store_words", 4, 1, 0),
+    ("store_scales", 2, 0, 0),
+    ("store_scales", 2, 1, 0),
+    ("store_scales", 2, 2, 0),
+    ("store_scales", 2, 3, 0),
 ]
 
 
@@ -271,26 +307,28 @@ def tile_koopman_control_step_g2_kernel(tc, phases, amp, koopman, control, u, dr
         unit32 = keep.tile([P, GROUPS, PACK], F32, name="unit32")
         bias32 = keep.tile([P, GROUPS, PACK], F32, name="bias32")
 
-        ph_raw = [[keep.tile([P, PACK, w], BF16, name="ph%d_%d" % (n, c)) for c in range(PSI_PASSES)] for n, w in enumerate(WIDTHS)]
-        u_raw = [keep.tile([P, PACK, w], BF16, name="u%d" % n) for n, w in enumerate(WIDTHS)]
-        w_raw = [ring("w_raw%d_" % g, PASSES, [P, PACK, K_PASS], BF16) for g in range(GROUPS)]
+        ph_raw = [[keep.tile([P, PACK, width(ns)], BF16, name="ph%d_%d" % (j, c)) for c in range(PSI_PASSES)] for j, ns in enumerate(LOADS)]
+        u_raw = [keep.tile([P, PACK, width(ns)], BF16, name="u%d" % j) for j, ns in enumerate(LOADS)]
         sin32 = ring("sin", SIN_BUFS, [P, PACK, BANK], F32)
         psi_bf = ring("psi_bf", PSI_BUFS, [P, PACK * BANK], BF16)
         u_bf = ring("u_bf", U_BUFS, [P, PACK * BANK], BF16)
-        w_bf = ring("w_bf", W_BUFS, [P, PACK * K_PASS], BF16)
-        y32 = ring("y32_", Y_BUFS, [P, PACK, BANK], F32)
+        y32 = [ring("y32_%d_" % j, GROUPS, [P, PACK, width(ns)], F32) for j, ns in enumerate(STORES)]
         y_bf = ring("y_bf", YB_BUFS, [P, PACK * BANK], BF16)
-        x_codes = [[keep.tile([P, w], U32, name="xc%d_%d" % (n, c), align_bytes=64) for c in range(PASSES)] for n, w in enumerate(WIDTHS)]
-        x_scales = [[keep.tile([P, w], U8, name="xs%d_%d" % (n, c), align_bytes=64) for c in range(PASSES)] for n, w in enumerate(WIDTHS)]
+        w_bf = ring("w_bf", W_BUFS, [P, PACK * K_PASS], BF16)
+        koop_raw, ctl_raw = y32[-2], y32[-1]
+        x_code_ring = [ring("xc%d_" % j, PASSES, [P, BANK], U32) for j in range(X_BUFS)]
+        x_scale_ring = [ring("xs%d_" % j, PASSES, [P, BANK], U8) for j in range(X_BUFS)]
+        x_codes = [[x_code_ring[n % X_BUFS][c][:, :w] for c in range(PASSES)] for n, w in enumerate(WIDTHS)]
+        x_scales = [[x_scale_ring[n % X_BUFS][c][:, :w] for c in range(PASSES)] for n, w in enumerate(WIDTHS)]
         w_codes = [ring("wc%d_" % g, PASSES, [P, K_PASS], U32) for g in range(GROUPS)]
         w_scales = [ring("ws%d_" % g, PASSES, [P, K_PASS], U8) for g in range(GROUPS)]
-        y_codes = [[keep.tile([P, w], U32, name="yc%d_%d" % (n, g), align_bytes=64) for g in range(GROUPS)] for n, w in enumerate(WIDTHS)]
-        early_width = STARTS[EARLY_CHUNKS]
-        y_scales_early = keep.tile([P, GROUPS, early_width], U8, name="ys_early", align_bytes=64)
-        y_scales_late = keep.tile([P, GROUPS, T - early_width], U8, name="ys_late", align_bytes=64)
+        y_codes = [ring("yc%d_" % j, GROUPS, [P, width(ns)], U32) for j, ns in enumerate(WORD_STORES)]
+        y_scales = [keep.tile([P, width(ns)], U8, name="ys%d" % j, align_bytes=64) for j, ns in enumerate(SCALE_STORES)]
 
         words_out = out_1.rearrange("g p m t -> g p (m t)").bitcast(I32)
         scales_out = out_2.bitcast(I32)
+
+        queues = [nc.sync, nc.scalar]
 
         def cols(n):
             return slice(STARTS[n], STARTS[n] + WIDTHS[n])
@@ -301,54 +339,65 @@ def tile_koopman_control_step_g2_kernel(tc, phases, amp, koopman, control, u, dr
         def load_vector(dst, src):
             nc.sync.dma_start(out=dst[:], in_=src.rearrange("(g p t) -> p g t", p=P, t=PACK))
 
-        def load_phases(n, c):
-            nc.sync.dma_start(out=ph_raw[n][c][:], in_=phases[rows(c), cols(n)].rearrange("(p t) m -> p t m", t=PACK))
+        def load_phases(j, c):
+            nc.sync.dma_start(out=ph_raw[j][c][:], in_=phases[rows(c), span(LOADS[j])].rearrange("(p t) m -> p t m", t=PACK))
 
-        def load_u(n):
-            nc.sync.dma_start(out=u_raw[n][:], in_=u[:, cols(n)].rearrange("(p t) m -> p t m", t=PACK))
+        def load_u(j):
+            nc.sync.dma_start(out=u_raw[j][:], in_=u[:, span(LOADS[j])].rearrange("(p t) m -> p t m", t=PACK))
 
-        def load_weight(g, c):
-            src = control[rows(g), :] if c == U_PASS else koopman[rows(g), rows(c)]
-            nc.sync.dma_start(out=w_raw[g][c][:], in_=src.rearrange("(p t) k -> p t k", t=PACK))
+        def load_koopman(g, half):
+            slots = slice(2 * half, 2 * half + 2)
+            nc.sync.dma_start(out=koop_raw[g][:, slots, :].bitcast(BF16), in_=koopman[rows(g), :].rearrange("(p t) k -> p t k", t=PACK)[:, slots, :])
+
+        def load_control(g):
+            nc.sync.dma_start(out=ctl_raw[g][:].bitcast(BF16), in_=control[rows(g), :].rearrange("(p t) k -> p t k", t=PACK))
 
         def interleaved(tile_bf, w, run):
             return tile_bf[:, : PACK * w].rearrange("p (b i t) -> p b t i", i=run, t=PACK)
 
-        def by_slot(tile, w, run):
-            return tile[:, :, :w].rearrange("p t (b i) -> p b t i", i=run)
+        def by_slot(tile, run):
+            return tile.rearrange("p t (b i) -> p b t i", i=run)
+
+        def interleave(dst, src, engine):
+            if engine == 0:
+                nc.vector.tensor_copy(out=dst, in_=src)
+            elif engine == 1:
+                nc.scalar.copy(out=dst, in_=src)
+            else:
+                nc.gpsimd.tensor_scalar(out=dst, in0=src, scalar1=1.0, scalar2=0.0, op0=ALU.mult, op1=ALU.add)
 
         def quantize(codes, scales, src):
             nc.vector.quantize_mx(out=codes.bitcast(FP8X4), scales=scales, in_=src)
 
         def sine(n, c):
+            group, inside = place(LOADS, n)
             j = PSI_PASSES * n + c
-            nc.scalar.activation(out=sin32[j % SIN_BUFS][:, :, : WIDTHS[n]], in_=ph_raw[n][c][:], func=ACT.Sin, bias=zero_bias[:])
+            nc.scalar.activation(out=sin32[j % SIN_BUFS][:, :, : WIDTHS[n]], in_=ph_raw[group][c][:, :, inside], func=ACT.Sin, bias=zero_bias[:])
 
         def times_amp(n, c):
             j, w = PSI_PASSES * n + c, WIDTHS[n]
             factor = amp_sb[:, c, :].unsqueeze(1).unsqueeze(3).to_broadcast([P, w // 2, PACK, 2])
-            nc.vector.tensor_tensor(out=interleaved(psi_bf[j % PSI_BUFS], w, 2), in0=by_slot(sin32[j % SIN_BUFS], w, 2), in1=factor, op=ALU.mult)
+            nc.vector.tensor_tensor(out=interleaved(psi_bf[j % PSI_BUFS], w, 2), in0=by_slot(sin32[j % SIN_BUFS][:, :, :w], 2), in1=factor, op=ALU.mult)
 
         def quantize_psi(n, c):
             j = PSI_PASSES * n + c
-            quantize(x_codes[n][c][:], x_scales[n][c][:], psi_bf[j % PSI_BUFS][:, : PACK * WIDTHS[n]])
+            quantize(x_codes[n][c], x_scales[n][c], psi_bf[j % PSI_BUFS][:, : PACK * WIDTHS[n]])
 
-        def interleave_u(n, on_scalar=False):
-            dst, src = interleaved(u_bf[n % U_BUFS], WIDTHS[n], 4), by_slot(u_raw[n], WIDTHS[n], 4)
-            if on_scalar:
-                nc.scalar.copy(out=dst, in_=src)
-            else:
-                nc.vector.tensor_copy(out=dst, in_=src)
+        def interleave_u(n, engine):
+            group, inside = place(LOADS, n)
+            dst, src = interleaved(u_bf[n % U_BUFS], WIDTHS[n], 4), by_slot(u_raw[group][:, :, inside], 4)
+            interleave(dst, src, engine)
 
         def quantize_u(n):
-            quantize(x_codes[n][U_PASS][:], x_scales[n][U_PASS][:], u_bf[n % U_BUFS][:, : PACK * WIDTHS[n]])
+            quantize(x_codes[n][U_PASS], x_scales[n][U_PASS], u_bf[n % U_BUFS][:, : PACK * WIDTHS[n]])
 
         W_BANKS = GROUPS * PASSES * 2
 
         def turn_weight(g, c, half):
             bank = banks[((g * PASSES + c) * 2 + half) % BANKS]
+            src = ctl_raw[g][:] if c == U_PASS else koop_raw[g][:, :, c * K_PASS // 2 : (c + 1) * K_PASS // 2]
             for s in range(2):
-                words = w_raw[g][c][:, 2 * half + s, :].bitcast(F32)
+                words = src[:, 2 * half + s, :]
                 for e in range(2):
                     at = (2 * s + e) * P
                     nc.tensor.transpose(bank[:, at : at + P], words[:, e : K_PASS // 2 : 2], ident[:])
@@ -366,7 +415,7 @@ def tile_koopman_control_step_g2_kernel(tc, phases, amp, koopman, control, u, dr
             quantize(w_codes[g][c][:], w_scales[g][c][:], w_bf[(g * PASSES + c) % W_BUFS][:])
 
         def acc_bank(n, g, t):
-            return banks[(W_BANKS + (GROUPS * n + g) * PACK + t) % BANKS][:, : WIDTHS[n]]
+            return banks[(W_BANKS + UNITS.index((n, g)) * PACK + t) % BANKS][:, : WIDTHS[n]]
 
         def multiply(n, g, t):
             m = slice(t * P, (t + 1) * P)
@@ -375,46 +424,47 @@ def tile_koopman_control_step_g2_kernel(tc, phases, amp, koopman, control, u, dr
                     out=acc_bank(n, g, t),
                     lhsT=w_codes[g][c][:, m].bitcast(FP8X4),
                     lhsT_scale=w_scales[g][c][:, m],
-                    rhs=x_codes[n][c][:].bitcast(FP8X4),
-                    rhs_scale=x_scales[n][c][:],
+                    rhs=x_codes[n][c].bitcast(FP8X4),
+                    rhs_scale=x_scales[n][c],
                     start=(c == 0),
                     stop=(c == PASSES - 1),
                 )
 
         def y_tile(n, g):
-            return y32[(GROUPS * n + g) % Y_BUFS]
+            group, inside = place(STORES, n)
+            return y32[group][g][:, :, inside]
 
         def finish(n, g, t, on_vector=False):
-            dst = y_tile(n, g)[:, t, : WIDTHS[n]]
+            dst = y_tile(n, g)[:, t, :]
             scale, bias = unit32[:, g, t : t + 1], bias32[:, g, t : t + 1]
             if on_vector:
                 nc.vector.tensor_scalar(out=dst, in0=acc_bank(n, g, t), scalar1=scale, scalar2=bias, op0=ALU.mult, op1=ALU.add)
             else:
                 nc.scalar.activation(out=dst, in_=acc_bank(n, g, t), func=ACT.Identity, bias=bias, scale=scale)
 
-        def store_y(n, g):
-            nc.sync.dma_start(out=out_0[rows(g), cols(n)].rearrange("(p t) m -> p t m", t=PACK), in_=y_tile(n, g)[:, :, : WIDTHS[n]])
+        def store_y(j, g, part, queue):
+            slots = slice(part * STORE_SLOTS, (part + 1) * STORE_SLOTS)
+            queues[queue].dma_start(out=out_0[rows(g), span(STORES[j])].rearrange("(p t) m -> p t m", t=PACK)[:, slots, :], in_=y32[j][g][:, slots, :])
 
-        def interleave_y(n, g):
+        def interleave_y(n, g, engine):
             w = WIDTHS[n]
-            nc.vector.tensor_copy(out=interleaved(y_bf[(GROUPS * n + g) % YB_BUFS], w, 2), in_=by_slot(y_tile(n, g), w, 2))
+            interleave(interleaved(y_bf[UNITS.index((n, g)) % YB_BUFS], w, 2), by_slot(y_tile(n, g), 2), engine)
 
         def quantize_y(n, g):
-            if n < EARLY_CHUNKS:
-                scales = y_scales_early[:, g, cols(n)]
-            else:
-                scales = y_scales_late[:, g, STARTS[n] - early_width : STARTS[n] - early_width + WIDTHS[n]]
-            quantize(y_codes[n][g][:], scales, y_bf[(GROUPS * n + g) % YB_BUFS][:, : PACK * WIDTHS[n]])
+            group, inside = place(SCALE_STORES, n)
+            scales = y_scales[group][4 * g :, inside]
+            group, inside = place(WORD_STORES, n)
+            quantize(y_codes[group][g][:, inside], scales, y_bf[UNITS.index((n, g)) % YB_BUFS][:, : PACK * WIDTHS[n]])
 
-        def store_words(n, g):
-            nc.sync.dma_start(out=words_out[g, :, cols(n)], in_=y_codes[n][g][:].bitcast(I32))
+        def store_words(j, g, queue):
+            queues[queue].dma_start(out=words_out[g, :, span(WORD_STORES[j])], in_=y_codes[j][g][:].bitcast(I32))
 
-        def store_scales(tile, first, last):
-            for q in range(4):
-                nc.sync.dma_start(
-                    out=scales_out[:, 4 * q : 4 * q + 4, first // 4 : last // 4].rearrange("g r m -> r g m"),
-                    in_=tile[32 * q : 32 * q + 4, :, :].bitcast(I32),
-                )
+        def store_scales(j, q, queue):
+            columns = span(SCALE_STORES[j])
+            queues[queue].dma_start(
+                out=scales_out[:, 4 * q : 4 * q + 4, columns.start // 4 : columns.stop // 4],
+                in_=y_scales[j][32 * q : 32 * q + 8, :].bitcast(I32),
+            )
 
         def prepare():
             nc.vector.memset(zero[:], 0.0)
@@ -432,15 +482,9 @@ def tile_koopman_control_step_g2_kernel(tc, phases, amp, koopman, control, u, dr
             nc.vector.tensor_copy(out=unit32[:], in_=unit_sb[:])
             nc.vector.tensor_tensor(out=bias32[:], in0=drift_sb[:], in1=unit_sb[:], op=ALU.mult)
 
-        def early_scales():
-            store_scales(y_scales_early, 0, early_width)
-
-        def late_scales():
-            store_scales(y_scales_late, early_width, T)
-
         steps = dict(
-            prepare=prepare, load_amp=load_amp, load_unit=load_unit, affine=affine, early_scales=early_scales, late_scales=late_scales,
-            load_phases=load_phases, load_u=load_u, load_weight=load_weight, sine=sine, times_amp=times_amp, quantize_psi=quantize_psi,
+            prepare=prepare, load_amp=load_amp, load_unit=load_unit, affine=affine, store_scales=store_scales,
+            load_phases=load_phases, load_u=load_u, load_koopman=load_koopman, load_control=load_control, sine=sine, times_amp=times_amp, quantize_psi=quantize_psi,
             interleave_u=interleave_u, quantize_u=quantize_u, turn_weight=turn_weight, copy_weight=copy_weight,
             quantize_weight=quantize_weight, multiply=multiply, finish=finish, store_y=store_y, interleave_y=interleave_y,
             quantize_y=quantize_y, store_words=store_words,

@@ -22,19 +22,22 @@ GROUPS = D // K_PASS
 PSI_PASSES = D // K_PASS
 U_PASS = PSI_PASSES
 PASSES = PSI_PASSES + 1
-BANKS = 8
+BANKS = 7
 BANK = 512
 WIDTHS = [256, 512, 512, 512, 256]
 STARTS = [sum(WIDTHS[:n]) for n in range(len(WIDTHS))]
 CHUNKS = len(WIDTHS)
 EARLY_CHUNKS = CHUNKS - 1
 SCALE_STORES = [[0, 1], [2, 3], [4]]
-LOADS = [[0], [1], [2, 3, 4]]
+LOADS = [[0], [1], [2], [3, 4]]
 STORES = [[0], [1], [2], [3], [4]]
 WORD_STORES = STORES
 STORE_SLOTS = 2
 UNITS = [(0,0),(1,0),(0,1),(1,1),(2,0),(2,1),(3,0),(3,1),(4,0),(4,1)]
-SIN_BUFS, PSI_BUFS, U_BUFS, YB_BUFS, X_BUFS, W_BUFS = 3, 3, 2, 3, 3, 2
+W_USERS = [[("w", g, c, half) for half in range(2) for c in range(PASSES)] for g in range(GROUPS)]
+Y_USERS = [[("y", n, g, t) for t in range(PACK)] for n, g in UNITS]
+USERS = W_USERS[0] + Y_USERS[0] + W_USERS[1] + sum(Y_USERS[1:], [])
+SIN_BUFS, PSI_BUFS, U_BUFS, YB_BUFS, X_BUFS, W_BUFS = 3, 3, 2, 2, 3, 3
 
 
 def span(chunks):
@@ -53,230 +56,243 @@ def width(chunks):
 
 
 ORDER = [
-    ("load_phases", 0, 0),
     ("prepare",),
+    ("load_phases", 0, 0),
     ("load_amp",),
-    ("load_phases", 0, 1),
-    ("load_phases", 1, 0),
     ("load_koopman", 0, 1),
-    ("load_koopman", 0, 0),
+    ("load_phases", 0, 1),
     ("load_phases", 1, 1),
     ("load_control", 0),
-    ("load_koopman", 1, 0),
-    ("load_koopman", 1, 1),
-    ("sine", 0, 0),
     ("load_u", 0),
-    ("sine", 0, 1),
-    ("times_amp", 0, 0),
+    ("load_koopman", 0, 0),
     ("load_u", 1),
-    ("sine", 1, 0),
-    ("times_amp", 0, 1),
-    ("load_control", 1),
-    ("turn_weight", 0, 0, 1),
-    ("quantize_psi", 0, 1),
-    ("quantize_psi", 0, 0),
-    ("load_phases", 2, 0),
-    ("turn_weight", 0, 0, 0),
-    ("times_amp", 1, 0),
-    ("copy_weight", 0, 0, 1, False),
-    ("turn_weight", 0, 1, 0),
+    ("sine", 0, 0),
+    ("load_koopman", 1, 0),
     ("load_unit",),
-    ("copy_weight", 0, 0, 0, False),
-    ("sine", 1, 1),
+    ("load_phases", 1, 0),
     ("turn_weight", 0, 1, 1),
-    ("quantize_weight", 0, 0),
-    ("quantize_psi", 1, 0),
-    ("turn_weight", 0, 2, 0),
-    ("load_phases", 2, 1),
-    ("copy_weight", 0, 1, 0, False),
-    ("turn_weight", 0, 2, 1),
-    ("times_amp", 1, 1),
-    ("copy_weight", 0, 2, 0, False),
+    ("times_amp", 0, 0),
     ("load_u", 2),
-    ("turn_weight", 1, 0, 0),
+    ("sine", 0, 1),
+    ("turn_weight", 0, 0, 1),
+    ("copy_weight", 0, 1, 1, True),
+    ("load_control", 1),
+    ("sine", 1, 1),
+    ("times_amp", 0, 1),
+    ("load_phases", 2, 0),
+    ("turn_weight", 0, 2, 0),
+    ("quantize_psi", 0, 0),
+    ("affine",),
+    ("load_koopman", 1, 1),
+    ("interleave_u", 0, 0, 0),
+    ("turn_weight", 0, 2, 1),
+    ("copy_weight", 0, 0, 1, False),
+    ("quantize_psi", 0, 1),
+    ("quantize_u", 0, 0),
+    ("copy_weight", 0, 2, 0, False),
+    ("interleave_u", 0, 1, 0),
+    ("load_phases", 2, 1),
+    ("turn_weight", 0, 0, 0),
+    ("quantize_u", 0, 1),
     ("copy_weight", 0, 2, 1, False),
-    ("copy_weight", 0, 1, 1, False),
-    ("turn_weight", 1, 0, 1),
-    ("interleave_u", 0, 1),
-    ("quantize_weight", 0, 1),
-    ("turn_weight", 1, 1, 1),
+    ("times_amp", 1, 1),
+    ("turn_weight", 0, 1, 0),
+    ("load_phases", 3, 1),
+    ("interleave_u", 1, 1, 1),
+    ("interleave_u", 1, 0, 2),
+    ("load_u", 3),
+    ("turn_weight", 1, 0, 0),
+    ("copy_weight", 0, 0, 0, False),
     ("quantize_weight", 0, 2),
-    ("copy_weight", 1, 0, 0, False),
-    ("interleave_u", 1, 0),
+    ("copy_weight", 0, 1, 0, False),
+    ("quantize_weight", 0, 0),
     ("turn_weight", 1, 1, 0),
-    ("copy_weight", 1, 0, 1, False),
-    ("copy_weight", 1, 1, 1, False),
-    ("turn_weight", 1, 2, 0),
-    ("quantize_weight", 1, 0),
-    ("copy_weight", 1, 1, 0, False),
-    ("quantize_u", 0),
-    ("quantize_u", 1),
-    ("turn_weight", 1, 2, 1),
-    ("copy_weight", 1, 2, 0, False),
+    ("load_phases", 3, 0),
+    ("sine", 1, 0),
+    ("quantize_weight", 0, 1),
+    ("multiply", 0, 0, 0),
+    ("quantize_u", 1, 0),
     ("quantize_psi", 1, 1),
     ("multiply", 0, 0, 2),
-    ("sine", 2, 0),
-    ("affine",),
-    ("multiply", 0, 0, 0),
-    ("copy_weight", 1, 2, 1, True),
+    ("quantize_u", 1, 1),
     ("multiply", 0, 0, 1),
-    ("quantize_weight", 1, 1),
+    ("copy_weight", 1, 0, 0, True),
+    ("interleave_u", 2, 0, 2),
+    ("copy_weight", 1, 1, 0, False),
     ("multiply", 0, 0, 3),
-    ("quantize_weight", 1, 2),
-    ("multiply", 1, 0, 1),
-    ("finish", 0, 0, 1, True),
+    ("times_amp", 1, 0),
+    ("finish", 0, 0, 1, False),
+    ("turn_weight", 1, 2, 0),
     ("finish", 0, 0, 2, False),
-    ("finish", 0, 0, 0, False),
-    ("times_amp", 2, 0),
-    ("multiply", 1, 0, 2),
     ("finish", 0, 0, 3, False),
-    ("finish", 1, 0, 1, False),
-    ("store_y", 0, 0, 0, 0),
-    ("multiply", 0, 1, 1),
+    ("interleave_u", 2, 1, 2),
+    ("turn_weight", 1, 2, 1),
+    ("sine", 2, 0),
     ("store_y", 0, 0, 1, 0),
-    ("sine", 2, 1),
-    ("multiply", 0, 1, 0),
-    ("multiply", 0, 1, 3),
+    ("finish", 0, 0, 0, True),
+    ("turn_weight", 1, 1, 1),
+    ("quantize_u", 2, 0),
+    ("quantize_psi", 1, 0),
+    ("store_y", 0, 0, 0, 0),
+    ("copy_weight", 1, 2, 1, True),
+    ("interleave_y", 0, 0, 2),
+    ("turn_weight", 1, 0, 1),
+    ("copy_weight", 1, 2, 0, False),
+    ("times_amp", 2, 0),
+    ("copy_weight", 1, 1, 1, False),
     ("multiply", 1, 0, 0),
-    ("interleave_y", 0, 0, 0),
-    ("finish", 0, 1, 1, True),
-    ("multiply", 0, 1, 2),
+    ("copy_weight", 1, 0, 1, False),
+    ("sine", 2, 1),
+    ("multiply", 1, 0, 2),
+    ("quantize_weight", 1, 0),
+    ("multiply", 1, 0, 1),
     ("quantize_y", 0, 0),
-    ("finish", 0, 1, 0, False),
-    ("quantize_psi", 2, 0),
+    ("quantize_weight", 1, 1),
     ("multiply", 1, 0, 3),
-    ("finish", 1, 0, 0, False),
     ("store_words", 0, 0, 0),
-    ("store_y", 0, 1, 0, 0),
+    ("finish", 1, 0, 0, False),
+    ("quantize_weight", 1, 2),
+    ("finish", 1, 0, 1, False),
     ("times_amp", 2, 1),
+    ("interleave_u", 3, 0, 2),
+    ("multiply", 0, 1, 0),
     ("finish", 1, 0, 2, False),
-    ("multiply", 1, 1, 0),
+    ("multiply", 0, 1, 3),
     ("store_y", 1, 0, 0, 0),
+    ("multiply", 0, 1, 2),
     ("finish", 1, 0, 3, False),
+    ("multiply", 0, 1, 1),
+    ("finish", 0, 1, 0, False),
     ("finish", 0, 1, 3, False),
-    ("multiply", 1, 1, 2),
-    ("finish", 0, 1, 2, False),
     ("store_y", 1, 0, 1, 0),
+    ("multiply", 1, 1, 0),
+    ("finish", 0, 1, 2, False),
+    ("quantize_psi", 2, 0),
     ("sine", 3, 0),
-    ("interleave_u", 2, 0),
-    ("multiply", 1, 1, 3),
+    ("quantize_u", 3, 0),
     ("store_y", 0, 1, 1, 0),
     ("multiply", 1, 1, 1),
+    ("finish", 0, 1, 1, True),
     ("quantize_psi", 2, 1),
-    ("quantize_u", 2),
-    ("multiply", 2, 0, 1),
-    ("finish", 1, 1, 3, False),
-    ("interleave_u", 3, 0),
-    ("finish", 1, 1, 2, False),
-    ("multiply", 2, 1, 3),
+    ("store_y", 0, 1, 0, 0),
+    ("multiply", 1, 1, 2),
+    ("interleave_y", 1, 0, 0),
     ("finish", 1, 1, 0, False),
-    ("store_y", 1, 1, 1, 0),
+    ("multiply", 1, 1, 3),
+    ("quantize_u", 2, 1),
     ("finish", 1, 1, 1, False),
-    ("times_amp", 3, 0),
-    ("multiply", 2, 1, 2),
+    ("quantize_y", 1, 0),
+    ("multiply", 2, 0, 1),
     ("sine", 3, 1),
+    ("times_amp", 3, 0),
+    ("interleave_u", 3, 1, 2),
     ("store_y", 1, 1, 0, 0),
+    ("store_words", 1, 0, 0),
     ("multiply", 2, 0, 0),
-    ("multiply", 2, 1, 0),
-    ("quantize_u", 3),
-    ("finish", 2, 1, 3, False),
-    ("multiply", 2, 1, 1),
+    ("interleave_u", 4, 0, 2),
+    ("multiply", 2, 0, 3),
+    ("finish", 1, 1, 3, False),
     ("times_amp", 3, 1),
-    ("finish", 2, 1, 2, False),
+    ("interleave_y", 0, 1, 2),
+    ("finish", 1, 1, 2, False),
     ("multiply", 2, 0, 2),
     ("finish", 2, 0, 0, False),
-    ("store_y", 2, 1, 1, 0),
+    ("store_y", 1, 1, 1, 0),
+    ("multiply", 2, 1, 2),
     ("finish", 2, 0, 1, False),
-    ("multiply", 2, 0, 3),
-    ("finish", 2, 1, 1, False),
+    ("finish", 2, 0, 2, False),
+    ("multiply", 2, 1, 3),
     ("quantize_psi", 3, 0),
     ("store_y", 2, 0, 0, 0),
-    ("finish", 2, 1, 0, False),
-    ("quantize_psi", 3, 1),
-    ("multiply", 3, 1, 2),
-    ("finish", 2, 0, 2, False),
-    ("interleave_y", 1, 0, 0),
-    ("store_y", 2, 1, 0, 0),
     ("finish", 2, 0, 3, False),
-    ("multiply", 3, 1, 3),
-    ("sine", 4, 1),
+    ("quantize_psi", 3, 1),
+    ("finish", 2, 1, 2, False),
+    ("multiply", 2, 1, 0),
+    ("quantize_u", 3, 1),
     ("store_y", 2, 0, 1, 0),
-    ("interleave_y", 0, 1, 0),
-    ("multiply", 3, 0, 3),
-    ("quantize_y", 1, 0),
-    ("finish", 3, 1, 2, False),
     ("interleave_y", 1, 1, 0),
-    ("finish", 3, 1, 3, False),
-    ("multiply", 3, 0, 2),
-    ("store_words", 1, 0, 0),
-    ("sine", 4, 0),
-    ("store_y", 3, 1, 1, 0),
-    ("multiply", 3, 1, 1),
+    ("finish", 2, 1, 3, False),
+    ("multiply", 2, 1, 1),
+    ("sine", 4, 1),
+    ("store_y", 2, 1, 1, 0),
     ("quantize_y", 0, 1),
+    ("multiply", 3, 0, 1),
     ("quantize_y", 1, 1),
-    ("finish", 3, 0, 3, False),
-    ("multiply", 3, 1, 0),
+    ("finish", 2, 1, 0, False),
     ("store_words", 0, 1, 0),
-    ("times_amp", 4, 1),
-    ("finish", 3, 0, 2, False),
+    ("finish", 2, 1, 1, True),
+    ("interleave_y", 2, 0, 2),
+    ("sine", 4, 0),
+    ("multiply", 3, 0, 0),
     ("store_words", 1, 1, 0),
     ("store_scales", 0, 0, 0),
     ("store_scales", 0, 1, 0),
-    ("multiply", 3, 0, 0),
+    ("times_amp", 4, 1),
     ("store_scales", 0, 2, 0),
-    ("interleave_u", 4, 1),
     ("store_scales", 0, 3, 0),
-    ("store_y", 3, 0, 1, 0),
-    ("times_amp", 4, 0),
-    ("multiply", 3, 0, 1),
-    ("finish", 3, 1, 1, False),
-    ("quantize_psi", 4, 1),
-    ("finish", 3, 1, 0, False),
-    ("quantize_psi", 4, 0),
-    ("quantize_u", 4),
-    ("finish", 3, 0, 0, False),
-    ("interleave_y", 2, 0, 0),
-    ("multiply", 4, 0, 3),
-    ("store_y", 3, 1, 0, 0),
-    ("multiply", 4, 1, 3),
+    ("store_y", 2, 1, 0, 0),
+    ("multiply", 3, 0, 2),
     ("finish", 3, 0, 1, False),
-    ("multiply", 4, 0, 2),
-    ("finish", 4, 0, 3, False),
-    ("interleave_y", 2, 1, 0),
-    ("multiply", 4, 0, 0),
-    ("finish", 4, 1, 3, False),
+    ("times_amp", 4, 0),
+    ("finish", 3, 0, 0, False),
+    ("multiply", 3, 0, 3),
+    ("finish", 3, 0, 2, False),
     ("store_y", 3, 0, 0, 0),
-    ("finish", 4, 0, 2, False),
+    ("quantize_psi", 4, 1),
+    ("multiply", 3, 1, 0),
+    ("quantize_y", 2, 0),
+    ("finish", 3, 0, 3, False),
+    ("interleave_y", 2, 1, 0),
+    ("interleave_u", 4, 1, 1),
+    ("multiply", 3, 1, 1),
+    ("store_words", 2, 0, 0),
+    ("store_y", 3, 0, 1, 0),
+    ("finish", 3, 1, 0, False),
+    ("multiply", 3, 1, 2),
+    ("quantize_psi", 4, 0),
+    ("finish", 3, 1, 1, False),
+    ("quantize_y", 2, 1),
+    ("multiply", 3, 1, 3),
+    ("interleave_y", 3, 0, 0),
+    ("store_y", 3, 1, 0, 0),
+    ("finish", 3, 1, 2, False),
+    ("store_words", 2, 1, 0),
+    ("finish", 3, 1, 3, False),
+    ("quantize_u", 4, 0),
+    ("quantize_u", 4, 1),
+    ("multiply", 4, 0, 1),
+    ("quantize_y", 3, 0),
+    ("multiply", 4, 0, 0),
+    ("store_y", 3, 1, 1, 0),
+    ("interleave_y", 3, 1, 0),
+    ("finish", 4, 0, 1, False),
+    ("store_words", 3, 0, 0),
     ("multiply", 4, 1, 1),
     ("finish", 4, 0, 0, False),
-    ("multiply", 4, 1, 2),
-    ("store_y", 4, 0, 1, 0),
-    ("interleave_y", 3, 0, 1),
-    ("quantize_y", 2, 0),
-    ("multiply", 4, 0, 1),
     ("multiply", 4, 1, 0),
-    ("finish", 4, 1, 2, True),
-    ("quantize_y", 2, 1),
-    ("store_words", 2, 0, 0),
-    ("store_y", 4, 1, 1, 0),
-    ("interleave_y", 3, 1, 0),
-    ("store_words", 2, 1, 0),
-    ("finish", 4, 0, 1, False),
-    ("interleave_y", 4, 0, 1),
-    ("quantize_y", 3, 0),
-    ("store_y", 4, 0, 0, 0),
-    ("quantize_y", 3, 1),
-    ("store_words", 3, 0, 0),
     ("finish", 4, 1, 1, False),
+    ("store_y", 4, 0, 0, 0),
+    ("multiply", 4, 0, 2),
+    ("quantize_y", 3, 1),
     ("finish", 4, 1, 0, False),
-    ("quantize_y", 4, 0),
+    ("multiply", 4, 1, 3),
+    ("store_y", 4, 1, 0, 0),
+    ("multiply", 4, 0, 3),
     ("store_words", 3, 1, 0),
     ("store_scales", 1, 0, 0),
+    ("finish", 4, 1, 3, False),
     ("store_scales", 1, 1, 0),
+    ("multiply", 4, 1, 2),
     ("store_scales", 1, 2, 0),
+    ("finish", 4, 0, 2, False),
+    ("finish", 4, 0, 3, True),
     ("store_scales", 1, 3, 0),
+    ("finish", 4, 1, 2, False),
+    ("interleave_y", 4, 0, 0),
+    ("store_y", 4, 0, 1, 0),
     ("interleave_y", 4, 1, 0),
-    ("store_y", 4, 1, 0, 0),
+    ("store_y", 4, 1, 1, 0),
+    ("quantize_y", 4, 0),
     ("quantize_y", 4, 1),
     ("store_words", 4, 0, 0),
     ("store_words", 4, 1, 0),
@@ -301,17 +317,17 @@ def tile_koopman_control_step_g2_kernel(tc, phases, amp, koopman, control, u, dr
         ident = keep.tile([P, P], F32, name="ident")
         zero = keep.tile([P, 1], F32, name="zero")
         zero_bias = keep.tile([P, 1], F32, name="zero_bias")
-        amp_sb = keep.tile([P, GROUPS, PACK], BF16, name="amp_sb")
-        drift_sb = keep.tile([P, GROUPS, PACK], BF16, name="drift_sb")
-        unit_sb = keep.tile([P, GROUPS, PACK], BF16, name="unit_sb")
-        unit32 = keep.tile([P, GROUPS, PACK], F32, name="unit32")
-        bias32 = keep.tile([P, GROUPS, PACK], F32, name="bias32")
+        ident_bf = keep.tile([P, P], BF16, name="ident_bf")
+        vec_rows = keep.tile([P, K_PASS], BF16, name="vec_rows")
+        vecs = psum.tile([P, PACK, P], BF16, name="vecs")
+        unit32 = keep.tile([P, PACK, GROUPS], F32, name="unit32")
+        bias32 = keep.tile([P, PACK, GROUPS], F32, name="bias32")
 
         ph_raw = [[keep.tile([P, PACK, width(ns)], BF16, name="ph%d_%d" % (j, c)) for c in range(PSI_PASSES)] for j, ns in enumerate(LOADS)]
         u_raw = [keep.tile([P, PACK, width(ns)], BF16, name="u%d" % j) for j, ns in enumerate(LOADS)]
         sin32 = ring("sin", SIN_BUFS, [P, PACK, BANK], F32)
         psi_bf = ring("psi_bf", PSI_BUFS, [P, PACK * BANK], BF16)
-        u_bf = ring("u_bf", U_BUFS, [P, PACK * BANK], BF16)
+        u_bf = ring("u_bf", 2, [P, PACK * BANK // 2], BF16)
         y32 = [ring("y32_%d_" % j, GROUPS, [P, PACK, width(ns)], F32) for j, ns in enumerate(STORES)]
         y_bf = ring("y_bf", YB_BUFS, [P, PACK * BANK], BF16)
         w_bf = ring("w_bf", W_BUFS, [P, PACK * K_PASS], BF16)
@@ -336,8 +352,8 @@ def tile_koopman_control_step_g2_kernel(tc, phases, amp, koopman, control, u, dr
         def rows(c):
             return slice(c * K_PASS, (c + 1) * K_PASS)
 
-        def load_vector(dst, src):
-            nc.sync.dma_start(out=dst[:], in_=src.rearrange("(g p t) -> p g t", p=P, t=PACK))
+        def load_vector(row, src):
+            nc.sync.dma_start(out=vec_rows[row : row + GROUPS, :], in_=src.rearrange("(g k) -> g k", g=GROUPS))
 
         def load_phases(j, c):
             nc.sync.dma_start(out=ph_raw[j][c][:], in_=phases[rows(c), span(LOADS[j])].rearrange("(p t) m -> p t m", t=PACK))
@@ -376,25 +392,26 @@ def tile_koopman_control_step_g2_kernel(tc, phases, amp, koopman, control, u, dr
 
         def times_amp(n, c):
             j, w = PSI_PASSES * n + c, WIDTHS[n]
-            factor = amp_sb[:, c, :].unsqueeze(1).unsqueeze(3).to_broadcast([P, w // 2, PACK, 2])
-            nc.vector.tensor_tensor(out=interleaved(psi_bf[j % PSI_BUFS], w, 2), in0=by_slot(sin32[j % SIN_BUFS][:, :, :w], 2), in1=factor, op=ALU.mult)
+            factor = vecs[:, :, c : c + 1].unsqueeze(1).to_broadcast([P, w // 4, PACK, 4])
+            nc.vector.tensor_tensor(out=interleaved(psi_bf[j % PSI_BUFS], w, 4), in0=by_slot(sin32[j % SIN_BUFS][:, :, :w], 4), in1=factor, op=ALU.mult)
 
         def quantize_psi(n, c):
             j = PSI_PASSES * n + c
             quantize(x_codes[n][c], x_scales[n][c], psi_bf[j % PSI_BUFS][:, : PACK * WIDTHS[n]])
 
-        def interleave_u(n, engine):
+        def interleave_u(n, half, engine):
             group, inside = place(LOADS, n)
-            dst, src = interleaved(u_bf[n % U_BUFS], WIDTHS[n], 4), by_slot(u_raw[group][:, :, inside], 4)
-            interleave(dst, src, engine)
+            w = WIDTHS[n] // 2
+            src = u_raw[group][:, :, inside][:, :, half * w : (half + 1) * w]
+            interleave(interleaved(u_bf[half], w, 4), by_slot(src, 4), engine)
 
-        def quantize_u(n):
-            quantize(x_codes[n][U_PASS], x_scales[n][U_PASS], u_bf[n % U_BUFS][:, : PACK * WIDTHS[n]])
-
-        W_BANKS = GROUPS * PASSES * 2
+        def quantize_u(n, half):
+            w = WIDTHS[n] // 2
+            part = slice(half * w, (half + 1) * w)
+            quantize(x_codes[n][U_PASS][:, part], x_scales[n][U_PASS][:, part], u_bf[half][:, : PACK * w])
 
         def turn_weight(g, c, half):
-            bank = banks[((g * PASSES + c) * 2 + half) % BANKS]
+            bank = banks[USERS.index(("w", g, c, half)) % BANKS]
             src = ctl_raw[g][:] if c == U_PASS else koop_raw[g][:, :, c * K_PASS // 2 : (c + 1) * K_PASS // 2]
             for s in range(2):
                 words = src[:, 2 * half + s, :]
@@ -403,7 +420,7 @@ def tile_koopman_control_step_g2_kernel(tc, phases, amp, koopman, control, u, dr
                     nc.tensor.transpose(bank[:, at : at + P], words[:, e : K_PASS // 2 : 2], ident[:])
 
         def copy_weight(g, c, half, on_vector=False):
-            bank = banks[((g * PASSES + c) * 2 + half) % BANKS]
+            bank = banks[USERS.index(("w", g, c, half)) % BANKS]
             dst = w_bf[(g * PASSES + c) % W_BUFS][:].bitcast(F32)[:, half * BANK : (half + 1) * BANK]
             dst, src = dst.rearrange("p (s m e) -> p s m e", s=2, e=2), bank[:].rearrange("p (s e m) -> p s m e", s=2, e=2)
             if on_vector:
@@ -415,7 +432,7 @@ def tile_koopman_control_step_g2_kernel(tc, phases, amp, koopman, control, u, dr
             quantize(w_codes[g][c][:], w_scales[g][c][:], w_bf[(g * PASSES + c) % W_BUFS][:])
 
         def acc_bank(n, g, t):
-            return banks[(W_BANKS + UNITS.index((n, g)) * PACK + t) % BANKS][:, : WIDTHS[n]]
+            return banks[USERS.index(("y", n, g, t)) % BANKS][:, : WIDTHS[n]]
 
         def multiply(n, g, t):
             m = slice(t * P, (t + 1) * P)
@@ -436,7 +453,7 @@ def tile_koopman_control_step_g2_kernel(tc, phases, amp, koopman, control, u, dr
 
         def finish(n, g, t, on_vector=False):
             dst = y_tile(n, g)[:, t, :]
-            scale, bias = unit32[:, g, t : t + 1], bias32[:, g, t : t + 1]
+            scale, bias = unit32[:, t, g : g + 1], bias32[:, t, g : g + 1]
             if on_vector:
                 nc.vector.tensor_scalar(out=dst, in0=acc_bank(n, g, t), scalar1=scale, scalar2=bias, op0=ALU.mult, op1=ALU.add)
             else:
@@ -448,7 +465,7 @@ def tile_koopman_control_step_g2_kernel(tc, phases, amp, koopman, control, u, dr
 
         def interleave_y(n, g, engine):
             w = WIDTHS[n]
-            interleave(interleaved(y_bf[UNITS.index((n, g)) % YB_BUFS], w, 2), by_slot(y_tile(n, g), 2), engine)
+            interleave(interleaved(y_bf[UNITS.index((n, g)) % YB_BUFS], w, 4), by_slot(y_tile(n, g), 4), engine)
 
         def quantize_y(n, g):
             group, inside = place(SCALE_STORES, n)
@@ -469,18 +486,22 @@ def tile_koopman_control_step_g2_kernel(tc, phases, amp, koopman, control, u, dr
         def prepare():
             nc.vector.memset(zero[:], 0.0)
             nc.scalar.activation(out=zero_bias[:], in_=zero[:], func=ACT.Sin)
+            nc.vector.memset(vec_rows[:], 0.0)
             make_identity(nc, ident[:])
+            nc.vector.tensor_copy(out=ident_bf[:], in_=ident[:])
 
         def load_amp():
-            load_vector(amp_sb, amp)
+            load_vector(0, amp)
+            load_vector(2, unit)
+            load_vector(4, drift)
 
         def load_unit():
-            load_vector(unit_sb, unit)
-            load_vector(drift_sb, drift)
+            for t in range(PACK):
+                nc.tensor.transpose(vecs[:, t, :], vec_rows[:, t::PACK], ident_bf[:])
 
         def affine():
-            nc.vector.tensor_copy(out=unit32[:], in_=unit_sb[:])
-            nc.vector.tensor_tensor(out=bias32[:], in0=drift_sb[:], in1=unit_sb[:], op=ALU.mult)
+            nc.vector.tensor_copy(out=unit32[:], in_=vecs[:, :, 2:4])
+            nc.vector.tensor_tensor(out=bias32[:], in0=vecs[:, :, 4:6], in1=unit32[:], op=ALU.mult)
 
         steps = dict(
             prepare=prepare, load_amp=load_amp, load_unit=load_unit, affine=affine, store_scales=store_scales,

@@ -28,7 +28,7 @@ WIDTHS = [256, 512, 512, 512, 256]
 STARTS = [sum(WIDTHS[:n]) for n in range(len(WIDTHS))]
 CHUNKS = len(WIDTHS)
 EARLY_CHUNKS = CHUNKS - 1
-SCALE_STORES = [[0, 1], [2, 3], [4]]
+SCALE_STORES = [[0, 1, 2], [3, 4]]
 LOADS = [[0], [1], [2], [3, 4]]
 STORES = [[0], [1], [2], [3], [4]]
 WORD_STORES = STORES
@@ -37,6 +37,8 @@ UNITS = [(0,0),(1,0),(0,1),(1,1),(2,0),(2,1),(3,0),(3,1),(4,0),(4,1)]
 W_USERS = [[("w", g, c, half) for half in range(2) for c in range(PASSES)] for g in range(GROUPS)]
 Y_USERS = [[("y", n, g, t) for t in range(PACK)] for n, g in UNITS]
 USERS = W_USERS[0] + Y_USERS[0] + W_USERS[1] + sum(Y_USERS[1:], [])
+SORTED = []
+SORT_BUFS = 3
 SIN_BUFS, PSI_BUFS, U_BUFS, YB_BUFS, X_BUFS, W_BUFS = 3, 3, 2, 2, 3, 3
 
 
@@ -56,250 +58,247 @@ def width(chunks):
 
 
 ORDER = [
-    ("prepare",),
-    ("load_phases", 0, 0),
-    ("load_amp",),
-    ("load_koopman", 0, 1),
-    ("load_phases", 0, 1),
-    ("load_phases", 1, 1),
-    ("load_control", 0),
-    ("load_u", 0),
     ("load_koopman", 0, 0),
+    ("prepare",),
+    ("load_amp",),
+    ("load_phases", 0, 0),
+    ("load_phases", 0, 1),
+    ("load_koopman", 0, 1),
+    ("load_phases", 1, 0),
+    ("load_control", 0),
+    ("turn_weight", 0, 1, 0),
+    ("load_koopman", 1, 0),
+    ("load_u", 0),
+    ("load_phases", 1, 1),
+    ("sort_vectors",),
     ("load_u", 1),
     ("sine", 0, 0),
-    ("load_koopman", 1, 0),
     ("load_unit",),
-    ("load_phases", 1, 0),
-    ("turn_weight", 0, 1, 1),
-    ("times_amp", 0, 0),
-    ("load_u", 2),
-    ("sine", 0, 1),
-    ("turn_weight", 0, 0, 1),
-    ("copy_weight", 0, 1, 1, True),
+    ("copy_weight", 0, 1, 0, True),
     ("load_control", 1),
-    ("sine", 1, 1),
+    ("turn_weight", 0, 0, 0),
+    ("affine",),
+    ("sine", 0, 1),
+    ("times_amp", 0, 0),
+    ("load_koopman", 1, 1),
+    ("turn_weight", 0, 1, 1),
+    ("copy_weight", 0, 0, 0, False),
     ("times_amp", 0, 1),
+    ("turn_weight", 0, 0, 1),
+    ("load_u", 2),
+    ("sine", 1, 0),
+    ("quantize_psi", 0, 0),
+    ("copy_weight", 0, 1, 1, True),
     ("load_phases", 2, 0),
     ("turn_weight", 0, 2, 0),
-    ("quantize_psi", 0, 0),
-    ("affine",),
-    ("load_koopman", 1, 1),
-    ("interleave_u", 0, 0, 0),
-    ("turn_weight", 0, 2, 1),
-    ("copy_weight", 0, 0, 1, False),
     ("quantize_psi", 0, 1),
-    ("quantize_u", 0, 0),
-    ("copy_weight", 0, 2, 0, False),
-    ("interleave_u", 0, 1, 0),
-    ("load_phases", 2, 1),
-    ("turn_weight", 0, 0, 0),
-    ("quantize_u", 0, 1),
-    ("copy_weight", 0, 2, 1, False),
-    ("times_amp", 1, 1),
-    ("turn_weight", 0, 1, 0),
-    ("load_phases", 3, 1),
-    ("interleave_u", 1, 1, 1),
-    ("interleave_u", 1, 0, 2),
-    ("load_u", 3),
-    ("turn_weight", 1, 0, 0),
-    ("copy_weight", 0, 0, 0, False),
-    ("quantize_weight", 0, 2),
-    ("copy_weight", 0, 1, 0, False),
-    ("quantize_weight", 0, 0),
-    ("turn_weight", 1, 1, 0),
-    ("load_phases", 3, 0),
-    ("sine", 1, 0),
     ("quantize_weight", 0, 1),
-    ("multiply", 0, 0, 0),
-    ("quantize_u", 1, 0),
-    ("quantize_psi", 1, 1),
-    ("multiply", 0, 0, 2),
-    ("quantize_u", 1, 1),
-    ("multiply", 0, 0, 1),
-    ("copy_weight", 1, 0, 0, True),
-    ("interleave_u", 2, 0, 2),
-    ("copy_weight", 1, 1, 0, False),
-    ("multiply", 0, 0, 3),
+    ("copy_weight", 0, 0, 1, False),
+    ("turn_weight", 0, 2, 1),
+    ("load_phases", 2, 1),
     ("times_amp", 1, 0),
-    ("finish", 0, 0, 1, False),
-    ("turn_weight", 1, 2, 0),
-    ("finish", 0, 0, 2, False),
-    ("finish", 0, 0, 3, False),
-    ("interleave_u", 2, 1, 2),
-    ("turn_weight", 1, 2, 1),
-    ("sine", 2, 0),
-    ("store_y", 0, 0, 1, 0),
-    ("finish", 0, 0, 0, True),
-    ("turn_weight", 1, 1, 1),
-    ("quantize_u", 2, 0),
+    ("copy_weight", 0, 2, 0, False),
+    ("load_u", 3),
+    ("interleave_u", 0, 0, 2),
+    ("turn_weight", 1, 1, 0),
+    ("copy_weight", 0, 2, 1, False),
+    ("interleave_u", 0, 1, 2),
+    ("load_phases", 3, 1),
+    ("turn_weight", 1, 0, 0),
+    ("sine", 1, 1),
+    ("quantize_u", 0, 0),
+    ("quantize_weight", 0, 0),
+    ("load_phases", 3, 0),
+    ("quantize_u", 0, 1),
+    ("quantize_weight", 0, 2),
+    ("multiply", 0, 0, 0),
     ("quantize_psi", 1, 0),
-    ("store_y", 0, 0, 0, 0),
-    ("copy_weight", 1, 2, 1, True),
-    ("interleave_y", 0, 0, 2),
+    ("interleave_u", 1, 1, 1),
+    ("multiply", 0, 0, 1),
+    ("interleave_u", 1, 0, 2),
+    ("copy_weight", 1, 0, 0, True),
+    ("multiply", 0, 0, 2),
+    ("finish", 0, 0, 0, True),
+    ("turn_weight", 1, 2, 0),
+    ("finish", 0, 0, 2, True),
+    ("copy_weight", 1, 1, 0, False),
+    ("finish", 0, 0, 1, False),
+    ("quantize_u", 1, 1),
     ("turn_weight", 1, 0, 1),
     ("copy_weight", 1, 2, 0, False),
-    ("times_amp", 2, 0),
-    ("copy_weight", 1, 1, 1, False),
-    ("multiply", 1, 0, 0),
+    ("times_amp", 1, 1),
+    ("store_y", 0, 0, 0, 0),
+    ("interleave_u", 2, 1, 2),
+    ("turn_weight", 1, 1, 1),
     ("copy_weight", 1, 0, 1, False),
-    ("sine", 2, 1),
-    ("multiply", 1, 0, 2),
+    ("sine", 2, 0),
+    ("turn_weight", 1, 2, 1),
+    ("quantize_u", 1, 0),
+    ("quantize_psi", 1, 1),
+    ("multiply", 0, 0, 3),
     ("quantize_weight", 1, 0),
-    ("multiply", 1, 0, 1),
-    ("quantize_y", 0, 0),
-    ("quantize_weight", 1, 1),
-    ("multiply", 1, 0, 3),
-    ("store_words", 0, 0, 0),
-    ("finish", 1, 0, 0, False),
-    ("quantize_weight", 1, 2),
-    ("finish", 1, 0, 1, False),
-    ("times_amp", 2, 1),
-    ("interleave_u", 3, 0, 2),
-    ("multiply", 0, 1, 0),
-    ("finish", 1, 0, 2, False),
-    ("multiply", 0, 1, 3),
-    ("store_y", 1, 0, 0, 0),
-    ("multiply", 0, 1, 2),
-    ("finish", 1, 0, 3, False),
-    ("multiply", 0, 1, 1),
-    ("finish", 0, 1, 0, False),
-    ("finish", 0, 1, 3, False),
-    ("store_y", 1, 0, 1, 0),
-    ("multiply", 1, 1, 0),
-    ("finish", 0, 1, 2, False),
-    ("quantize_psi", 2, 0),
-    ("sine", 3, 0),
-    ("quantize_u", 3, 0),
-    ("store_y", 0, 1, 1, 0),
-    ("multiply", 1, 1, 1),
-    ("finish", 0, 1, 1, True),
-    ("quantize_psi", 2, 1),
-    ("store_y", 0, 1, 0, 0),
-    ("multiply", 1, 1, 2),
-    ("interleave_y", 1, 0, 0),
-    ("finish", 1, 1, 0, False),
-    ("multiply", 1, 1, 3),
+    ("multiply", 1, 0, 2),
+    ("copy_weight", 1, 2, 1, False),
+    ("copy_weight", 1, 1, 1, True),
+    ("finish", 0, 0, 3, False),
     ("quantize_u", 2, 1),
-    ("finish", 1, 1, 1, False),
-    ("quantize_y", 1, 0),
-    ("multiply", 2, 0, 1),
-    ("sine", 3, 1),
-    ("times_amp", 3, 0),
+    ("multiply", 1, 0, 3),
+    ("finish", 1, 0, 2, False),
+    ("quantize_weight", 1, 1),
+    ("store_y", 0, 0, 1, 0),
+    ("sine", 2, 1),
+    ("quantize_weight", 1, 2),
+    ("multiply", 1, 0, 1),
+    ("interleave_y", 0, 0, 2),
+    ("finish", 1, 0, 3, True),
+    ("times_amp", 2, 0),
+    ("store_y", 1, 0, 1, 0),
+    ("multiply", 1, 0, 0),
+    ("finish", 1, 0, 1, False),
+    ("interleave_u", 2, 0, 2),
+    ("multiply", 0, 1, 2),
+    ("finish", 1, 0, 0, False),
+    ("multiply", 1, 1, 1),
+    ("store_y", 1, 0, 0, 0),
+    ("times_amp", 2, 1),
     ("interleave_u", 3, 1, 2),
+    ("multiply", 1, 1, 0),
+    ("finish", 1, 1, 1, False),
+    ("finish", 0, 1, 2, False),
+    ("multiply", 0, 1, 3),
+    ("finish", 1, 1, 0, False),
+    ("quantize_y", 0, 0),
+    ("multiply", 0, 1, 1),
+    ("sine", 3, 0),
+    ("quantize_u", 2, 0),
     ("store_y", 1, 1, 0, 0),
-    ("store_words", 1, 0, 0),
+    ("store_words", 0, 0, 0),
+    ("quantize_psi", 2, 1),
+    ("multiply", 1, 1, 2),
+    ("quantize_psi", 2, 0),
+    ("multiply", 0, 1, 0),
+    ("interleave_u", 3, 0, 2),
+    ("finish", 0, 1, 3, True),
+    ("finish", 0, 1, 1, True),
+    ("store_y", 0, 1, 1, 0),
+    ("multiply", 2, 1, 0),
+    ("sine", 3, 1),
+    ("finish", 0, 1, 0, True),
+    ("times_amp", 3, 0),
+    ("store_y", 0, 1, 0, 0),
+    ("interleave_y", 1, 0, 2),
+    ("multiply", 1, 1, 3),
     ("multiply", 2, 0, 0),
-    ("interleave_u", 4, 0, 2),
-    ("multiply", 2, 0, 3),
-    ("finish", 1, 1, 3, False),
-    ("times_amp", 3, 1),
-    ("interleave_y", 0, 1, 2),
     ("finish", 1, 1, 2, False),
-    ("multiply", 2, 0, 2),
+    ("times_amp", 3, 1),
+    ("finish", 1, 1, 3, False),
+    ("multiply", 2, 0, 1),
     ("finish", 2, 0, 0, False),
     ("store_y", 1, 1, 1, 0),
-    ("multiply", 2, 1, 2),
+    ("multiply", 2, 0, 2),
     ("finish", 2, 0, 1, False),
-    ("finish", 2, 0, 2, False),
-    ("multiply", 2, 1, 3),
+    ("interleave_y", 0, 1, 1),
     ("quantize_psi", 3, 0),
     ("store_y", 2, 0, 0, 0),
-    ("finish", 2, 0, 3, False),
-    ("quantize_psi", 3, 1),
-    ("finish", 2, 1, 2, False),
-    ("multiply", 2, 1, 0),
-    ("quantize_u", 3, 1),
-    ("store_y", 2, 0, 1, 0),
-    ("interleave_y", 1, 1, 0),
-    ("finish", 2, 1, 3, False),
     ("multiply", 2, 1, 1),
-    ("sine", 4, 1),
-    ("store_y", 2, 1, 1, 0),
-    ("quantize_y", 0, 1),
-    ("multiply", 3, 0, 1),
-    ("quantize_y", 1, 1),
+    ("quantize_y", 1, 0),
+    ("quantize_u", 3, 0),
+    ("store_words", 1, 0, 0),
     ("finish", 2, 1, 0, False),
+    ("quantize_y", 0, 1),
+    ("multiply", 2, 0, 3),
+    ("interleave_y", 1, 1, 0),
     ("store_words", 0, 1, 0),
-    ("finish", 2, 1, 1, True),
-    ("interleave_y", 2, 0, 2),
-    ("sine", 4, 0),
-    ("multiply", 3, 0, 0),
-    ("store_words", 1, 1, 0),
-    ("store_scales", 0, 0, 0),
-    ("store_scales", 0, 1, 0),
-    ("times_amp", 4, 1),
-    ("store_scales", 0, 2, 0),
-    ("store_scales", 0, 3, 0),
+    ("finish", 2, 1, 1, False),
+    ("finish", 2, 0, 2, False),
+    ("multiply", 2, 1, 3),
     ("store_y", 2, 1, 0, 0),
-    ("multiply", 3, 0, 2),
-    ("finish", 3, 0, 1, False),
-    ("times_amp", 4, 0),
-    ("finish", 3, 0, 0, False),
+    ("quantize_psi", 3, 1),
+    ("finish", 2, 0, 3, False),
+    ("quantize_u", 3, 1),
+    ("quantize_y", 1, 1),
+    ("multiply", 2, 1, 2),
+    ("finish", 2, 1, 3, False),
+    ("store_y", 2, 0, 1, 0),
+    ("interleave_y", 2, 0, 0),
+    ("store_words", 1, 1, 0),
     ("multiply", 3, 0, 3),
-    ("finish", 3, 0, 2, False),
-    ("store_y", 3, 0, 0, 0),
-    ("quantize_psi", 4, 1),
-    ("multiply", 3, 1, 0),
-    ("quantize_y", 2, 0),
+    ("finish", 2, 1, 2, False),
+    ("interleave_u", 4, 0, 2),
+    ("store_y", 2, 1, 1, 0),
+    ("multiply", 3, 0, 2),
     ("finish", 3, 0, 3, False),
     ("interleave_y", 2, 1, 0),
-    ("interleave_u", 4, 1, 1),
-    ("multiply", 3, 1, 1),
-    ("store_words", 2, 0, 0),
+    ("multiply", 3, 0, 0),
+    ("finish", 3, 0, 2, False),
+    ("quantize_y", 2, 0),
+    ("sine", 4, 0),
     ("store_y", 3, 0, 1, 0),
-    ("finish", 3, 1, 0, False),
+    ("interleave_u", 4, 1, 2),
+    ("store_words", 2, 0, 0),
+    ("multiply", 3, 0, 1),
+    ("finish", 3, 0, 0, True),
+    ("times_amp", 4, 0),
     ("multiply", 3, 1, 2),
-    ("quantize_psi", 4, 0),
-    ("finish", 3, 1, 1, False),
+    ("finish", 3, 0, 1, False),
+    ("sine", 4, 1),
+    ("store_y", 3, 0, 0, 0),
     ("quantize_y", 2, 1),
     ("multiply", 3, 1, 3),
-    ("interleave_y", 3, 0, 0),
-    ("store_y", 3, 1, 0, 0),
-    ("finish", 3, 1, 2, False),
-    ("store_words", 2, 1, 0),
-    ("finish", 3, 1, 3, False),
     ("quantize_u", 4, 0),
-    ("quantize_u", 4, 1),
-    ("multiply", 4, 0, 1),
-    ("quantize_y", 3, 0),
-    ("multiply", 4, 0, 0),
+    ("store_scales", 0, 2, 0),
+    ("store_scales", 0, 3, 0),
+    ("store_words", 2, 1, 0),
+    ("times_amp", 4, 1),
+    ("store_scales", 0, 0, 0),
+    ("multiply", 3, 1, 1),
+    ("finish", 3, 1, 3, False),
+    ("finish", 3, 1, 2, False),
+    ("quantize_psi", 4, 0),
+    ("multiply", 3, 1, 0),
+    ("quantize_psi", 4, 1),
+    ("finish", 3, 1, 1, False),
     ("store_y", 3, 1, 1, 0),
-    ("interleave_y", 3, 1, 0),
-    ("finish", 4, 0, 1, False),
-    ("store_words", 3, 0, 0),
-    ("multiply", 4, 1, 1),
+    ("quantize_u", 4, 1),
+    ("store_scales", 0, 1, 0),
+    ("interleave_y", 3, 0, 0),
+    ("multiply", 4, 0, 0),
+    ("finish", 3, 1, 0, False),
+    ("multiply", 4, 0, 1),
     ("finish", 4, 0, 0, False),
+    ("quantize_y", 3, 0),
+    ("store_y", 3, 1, 0, 0),
+    ("multiply", 4, 0, 2),
+    ("finish", 4, 0, 1, False),
+    ("interleave_y", 3, 1, 0),
+    ("store_y", 4, 0, 0, 0),
+    ("multiply", 4, 0, 3),
+    ("store_words", 3, 0, 0),
+    ("finish", 4, 0, 2, False),
+    ("multiply", 4, 1, 1),
+    ("finish", 4, 0, 3, False),
+    ("store_y", 4, 0, 1, 0),
+    ("interleave_y", 4, 0, 0),
     ("multiply", 4, 1, 0),
     ("finish", 4, 1, 1, False),
-    ("store_y", 4, 0, 0, 0),
-    ("multiply", 4, 0, 2),
     ("quantize_y", 3, 1),
-    ("finish", 4, 1, 0, False),
-    ("multiply", 4, 1, 3),
-    ("store_y", 4, 1, 0, 0),
-    ("multiply", 4, 0, 3),
-    ("store_words", 3, 1, 0),
-    ("store_scales", 1, 0, 0),
-    ("finish", 4, 1, 3, False),
-    ("store_scales", 1, 1, 0),
     ("multiply", 4, 1, 2),
-    ("store_scales", 1, 2, 0),
-    ("finish", 4, 0, 2, False),
-    ("finish", 4, 0, 3, True),
-    ("store_scales", 1, 3, 0),
-    ("finish", 4, 1, 2, False),
-    ("interleave_y", 4, 0, 0),
-    ("store_y", 4, 0, 1, 0),
-    ("interleave_y", 4, 1, 0),
-    ("store_y", 4, 1, 1, 0),
+    ("finish", 4, 1, 0, False),
+    ("store_y", 4, 1, 0, 0),
     ("quantize_y", 4, 0),
+    ("multiply", 4, 1, 3),
+    ("store_words", 3, 1, 0),
+    ("finish", 4, 1, 2, False),
+    ("finish", 4, 1, 3, False),
+    ("store_words", 4, 0, 1),
+    ("store_y", 4, 1, 1, 0),
+    ("interleave_y", 4, 1, 0),
     ("quantize_y", 4, 1),
-    ("store_words", 4, 0, 0),
-    ("store_words", 4, 1, 0),
-    ("store_scales", 2, 0, 0),
-    ("store_scales", 2, 1, 0),
-    ("store_scales", 2, 2, 0),
-    ("store_scales", 2, 3, 0),
+    ("store_words", 4, 1, 1),
+    ("store_scales", 1, 3, 0),
+    ("store_scales", 1, 1, 0),
+    ("store_scales", 1, 2, 1),
+    ("store_scales", 1, 0, 1),
 ]
 
 
@@ -319,6 +318,7 @@ def tile_koopman_control_step_g2_kernel(tc, phases, amp, koopman, control, u, dr
         zero_bias = keep.tile([P, 1], F32, name="zero_bias")
         ident_bf = keep.tile([P, P], BF16, name="ident_bf")
         vec_rows = keep.tile([P, K_PASS], BF16, name="vec_rows")
+        vec_sorted = keep.tile([P, PACK, P], BF16, name="vec_sorted")
         vecs = psum.tile([P, PACK, P], BF16, name="vecs")
         unit32 = keep.tile([P, PACK, GROUPS], F32, name="unit32")
         bias32 = keep.tile([P, PACK, GROUPS], F32, name="bias32")
@@ -332,6 +332,7 @@ def tile_koopman_control_step_g2_kernel(tc, phases, amp, koopman, control, u, dr
         y_bf = ring("y_bf", YB_BUFS, [P, PACK * BANK], BF16)
         w_bf = ring("w_bf", W_BUFS, [P, PACK * K_PASS], BF16)
         koop_raw, ctl_raw = y32[-2], y32[-1]
+        w_sorted = ring("w_sorted", SORT_BUFS, [P, 2, 2, P], F32)
         x_code_ring = [ring("xc%d_" % j, PASSES, [P, BANK], U32) for j in range(X_BUFS)]
         x_scale_ring = [ring("xs%d_" % j, PASSES, [P, BANK], U8) for j in range(X_BUFS)]
         x_codes = [[x_code_ring[n % X_BUFS][c][:, :w] for c in range(PASSES)] for n, w in enumerate(WIDTHS)]
@@ -410,14 +411,28 @@ def tile_koopman_control_step_g2_kernel(tc, phases, amp, koopman, control, u, dr
             part = slice(half * w, (half + 1) * w)
             quantize(x_codes[n][U_PASS][:, part], x_scales[n][U_PASS][:, part], u_bf[half][:, : PACK * w])
 
+        def weight_words(g, c, half):
+            src = ctl_raw[g][:] if c == U_PASS else koop_raw[g][:, :, c * K_PASS // 2 : (c + 1) * K_PASS // 2]
+            return src[:, 2 * half : 2 * half + 2, :]
+
+        def sort_weight(g, c, half, on_scalar):
+            dst = w_sorted[SORTED.index(("w", g, c, half)) % SORT_BUFS][:]
+            src = weight_words(g, c, half).rearrange("p s (q e) -> p s e q", e=2)
+            if on_scalar:
+                nc.scalar.copy(out=dst, in_=src)
+            else:
+                nc.vector.tensor_copy(out=dst, in_=src)
+
         def turn_weight(g, c, half):
             bank = banks[USERS.index(("w", g, c, half)) % BANKS]
-            src = ctl_raw[g][:] if c == U_PASS else koop_raw[g][:, :, c * K_PASS // 2 : (c + 1) * K_PASS // 2]
             for s in range(2):
-                words = src[:, 2 * half + s, :]
                 for e in range(2):
                     at = (2 * s + e) * P
-                    nc.tensor.transpose(bank[:, at : at + P], words[:, e : K_PASS // 2 : 2], ident[:])
+                    if ("w", g, c, half) in SORTED:
+                        src = w_sorted[SORTED.index(("w", g, c, half)) % SORT_BUFS][:, s, e, :]
+                    else:
+                        src = weight_words(g, c, half)[:, s, e::2]
+                    nc.tensor.transpose(bank[:, at : at + P], src, ident[:])
 
         def copy_weight(g, c, half, on_vector=False):
             bank = banks[USERS.index(("w", g, c, half)) % BANKS]
@@ -495,9 +510,12 @@ def tile_koopman_control_step_g2_kernel(tc, phases, amp, koopman, control, u, dr
             load_vector(2, unit)
             load_vector(4, drift)
 
+        def sort_vectors():
+            nc.vector.tensor_copy(out=vec_sorted[:], in_=vec_rows[:].rearrange("r (p t) -> r t p", t=PACK))
+
         def load_unit():
             for t in range(PACK):
-                nc.tensor.transpose(vecs[:, t, :], vec_rows[:, t::PACK], ident_bf[:])
+                nc.tensor.transpose(vecs[:, t, :], vec_sorted[:, t, :], ident_bf[:])
 
         def affine():
             nc.vector.tensor_copy(out=unit32[:], in_=vecs[:, :, 2:4])
@@ -506,7 +524,7 @@ def tile_koopman_control_step_g2_kernel(tc, phases, amp, koopman, control, u, dr
         steps = dict(
             prepare=prepare, load_amp=load_amp, load_unit=load_unit, affine=affine, store_scales=store_scales,
             load_phases=load_phases, load_u=load_u, load_koopman=load_koopman, load_control=load_control, sine=sine, times_amp=times_amp, quantize_psi=quantize_psi,
-            interleave_u=interleave_u, quantize_u=quantize_u, turn_weight=turn_weight, copy_weight=copy_weight,
+            interleave_u=interleave_u, quantize_u=quantize_u, turn_weight=turn_weight, sort_weight=sort_weight, sort_vectors=sort_vectors, copy_weight=copy_weight,
             quantize_weight=quantize_weight, multiply=multiply, finish=finish, store_y=store_y, interleave_y=interleave_y,
             quantize_y=quantize_y, store_words=store_words,
         )

@@ -66,239 +66,239 @@ ORDER = [
     ("load_koopman", 0, 1),
     ("load_phases", 1, 0),
     ("load_control", 0),
-    ("turn_weight", 0, 1, 0),
     ("load_koopman", 1, 0),
+    ("turn_weight", 0, 1, 0),
     ("load_u", 0),
     ("load_phases", 1, 1),
     ("sort_vectors",),
-    ("load_u", 1),
+    ("load_control", 1),
     ("sine", 0, 0),
     ("load_unit",),
     ("copy_weight", 0, 1, 0, True),
-    ("load_control", 1),
+    ("load_u", 1),
     ("turn_weight", 0, 0, 0),
     ("affine",),
     ("sine", 0, 1),
     ("times_amp", 0, 0),
-    ("load_koopman", 1, 1),
+    ("load_phases", 2, 0),
     ("turn_weight", 0, 1, 1),
     ("copy_weight", 0, 0, 0, False),
     ("times_amp", 0, 1),
-    ("turn_weight", 0, 0, 1),
-    ("load_u", 2),
+    ("load_koopman", 1, 1),
     ("sine", 1, 0),
+    ("turn_weight", 0, 0, 1),
+    ("load_u", 3),
     ("quantize_psi", 0, 0),
     ("copy_weight", 0, 1, 1, True),
-    ("load_phases", 2, 0),
     ("turn_weight", 0, 2, 0),
     ("quantize_psi", 0, 1),
-    ("quantize_weight", 0, 1),
-    ("copy_weight", 0, 0, 1, False),
-    ("turn_weight", 0, 2, 1),
     ("load_phases", 2, 1),
-    ("times_amp", 1, 0),
+    ("quantize_weight", 0, 1),
+    ("turn_weight", 0, 2, 1),
+    ("load_phases", 3, 0),
     ("copy_weight", 0, 2, 0, False),
-    ("load_u", 3),
+    ("times_amp", 1, 0),
     ("interleave_u", 0, 0, 2),
+    ("copy_weight", 0, 0, 1, False),
     ("turn_weight", 1, 1, 0),
-    ("copy_weight", 0, 2, 1, False),
     ("interleave_u", 0, 1, 2),
-    ("load_phases", 3, 1),
-    ("turn_weight", 1, 0, 0),
+    ("copy_weight", 0, 2, 1, False),
+    ("load_u", 2),
     ("sine", 1, 1),
+    ("turn_weight", 1, 0, 0),
+    ("load_phases", 3, 1),
     ("quantize_u", 0, 0),
     ("quantize_weight", 0, 0),
-    ("load_phases", 3, 0),
-    ("quantize_u", 0, 1),
-    ("quantize_weight", 0, 2),
-    ("multiply", 0, 0, 0),
-    ("quantize_psi", 1, 0),
-    ("interleave_u", 1, 1, 1),
-    ("multiply", 0, 0, 1),
-    ("interleave_u", 1, 0, 2),
-    ("copy_weight", 1, 0, 0, True),
-    ("multiply", 0, 0, 2),
-    ("finish", 0, 0, 0, True),
     ("turn_weight", 1, 2, 0),
-    ("finish", 0, 0, 2, True),
-    ("copy_weight", 1, 1, 0, False),
-    ("finish", 0, 0, 1, False),
-    ("quantize_u", 1, 1),
-    ("turn_weight", 1, 0, 1),
+    ("quantize_weight", 0, 2),
+    ("quantize_u", 0, 1),
+    ("quantize_psi", 1, 0),
+    ("multiply", 0, 0, 2),
     ("copy_weight", 1, 2, 0, False),
+    ("copy_weight", 1, 0, 0, True),
+    ("interleave_u", 1, 1, 2),
+    ("multiply", 0, 0, 1),
+    ("finish", 0, 0, 2, False),
     ("times_amp", 1, 1),
-    ("store_y", 0, 0, 0, 0),
-    ("interleave_u", 2, 1, 2),
-    ("turn_weight", 1, 1, 1),
-    ("copy_weight", 1, 0, 1, False),
+    ("multiply", 0, 0, 0),
+    ("finish", 0, 0, 1, False),
     ("sine", 2, 0),
-    ("turn_weight", 1, 2, 1),
-    ("quantize_u", 1, 0),
-    ("quantize_psi", 1, 1),
     ("multiply", 0, 0, 3),
-    ("quantize_weight", 1, 0),
-    ("multiply", 1, 0, 2),
-    ("copy_weight", 1, 2, 1, False),
+    ("interleave_u", 1, 0, 2),
+    ("turn_weight", 1, 1, 1),
+    ("turn_weight", 1, 2, 1),
+    ("finish", 0, 0, 0, True),
     ("copy_weight", 1, 1, 1, True),
-    ("finish", 0, 0, 3, False),
-    ("quantize_u", 2, 1),
-    ("multiply", 1, 0, 3),
-    ("finish", 1, 0, 2, False),
-    ("quantize_weight", 1, 1),
-    ("store_y", 0, 0, 1, 0),
-    ("sine", 2, 1),
+    ("quantize_psi", 1, 1),
+    ("turn_weight", 1, 0, 1),
+    ("copy_weight", 1, 2, 1, False),
+    ("quantize_u", 1, 1),
+    ("copy_weight", 1, 1, 0, False),
+    ("quantize_u", 1, 0),
     ("quantize_weight", 1, 2),
-    ("multiply", 1, 0, 1),
-    ("interleave_y", 0, 0, 2),
+    ("multiply", 1, 0, 3),
+    ("copy_weight", 1, 0, 1, False),
+    ("quantize_weight", 1, 1),
+    ("finish", 0, 0, 3, False),
+    ("multiply", 1, 0, 2),
+    ("sine", 2, 1),
+    ("quantize_weight", 1, 0),
+    ("store_y", 0, 0, 1, 0),
+    ("store_y", 0, 0, 0, 0),
     ("finish", 1, 0, 3, True),
+    ("interleave_y", 0, 0, 2),
+    ("multiply", 1, 0, 1),
     ("times_amp", 2, 0),
+    ("interleave_u", 2, 0, 2),
+    ("multiply", 0, 1, 0),
+    ("finish", 1, 0, 2, False),
+    ("multiply", 0, 1, 1),
+    ("finish", 1, 0, 1, False),
     ("store_y", 1, 0, 1, 0),
     ("multiply", 1, 0, 0),
-    ("finish", 1, 0, 1, False),
-    ("interleave_u", 2, 0, 2),
+    ("finish", 0, 1, 0, False),
+    ("interleave_u", 2, 1, 2),
+    ("finish", 0, 1, 1, True),
+    ("times_amp", 2, 1),
+    ("store_y", 0, 1, 0, 0),
     ("multiply", 0, 1, 2),
     ("finish", 1, 0, 0, False),
-    ("multiply", 1, 1, 1),
-    ("store_y", 1, 0, 0, 0),
-    ("times_amp", 2, 1),
-    ("interleave_u", 3, 1, 2),
     ("multiply", 1, 1, 0),
-    ("finish", 1, 1, 1, False),
-    ("finish", 0, 1, 2, False),
-    ("multiply", 0, 1, 3),
-    ("finish", 1, 1, 0, False),
-    ("quantize_y", 0, 0),
-    ("multiply", 0, 1, 1),
     ("sine", 3, 0),
+    ("store_y", 1, 0, 0, 0),
+    ("multiply", 0, 1, 3),
+    ("multiply", 1, 1, 1),
+    ("quantize_y", 0, 0),
     ("quantize_u", 2, 0),
-    ("store_y", 1, 1, 0, 0),
     ("store_words", 0, 0, 0),
+    ("quantize_u", 2, 1),
     ("quantize_psi", 2, 1),
+    ("finish", 0, 1, 3, False),
     ("multiply", 1, 1, 2),
-    ("quantize_psi", 2, 0),
-    ("multiply", 0, 1, 0),
-    ("interleave_u", 3, 0, 2),
-    ("finish", 0, 1, 3, True),
-    ("finish", 0, 1, 1, True),
+    ("finish", 0, 1, 2, False),
+    ("interleave_u", 3, 1, 0),
+    ("finish", 1, 1, 1, False),
     ("store_y", 0, 1, 1, 0),
-    ("multiply", 2, 1, 0),
-    ("sine", 3, 1),
-    ("finish", 0, 1, 0, True),
-    ("times_amp", 3, 0),
-    ("store_y", 0, 1, 0, 0),
-    ("interleave_y", 1, 0, 2),
     ("multiply", 1, 1, 3),
+    ("quantize_psi", 2, 0),
+    ("finish", 1, 1, 0, False),
+    ("sine", 3, 1),
+    ("quantize_u", 3, 1),
+    ("store_y", 1, 1, 0, 0),
+    ("times_amp", 3, 0),
+    ("interleave_u", 3, 0, 2),
+    ("multiply", 2, 0, 1),
     ("multiply", 2, 0, 0),
+    ("interleave_y", 1, 0, 2),
+    ("finish", 1, 1, 3, False),
+    ("multiply", 2, 1, 0),
+    ("finish", 2, 0, 1, True),
     ("finish", 1, 1, 2, False),
     ("times_amp", 3, 1),
-    ("finish", 1, 1, 3, False),
-    ("multiply", 2, 0, 1),
     ("finish", 2, 0, 0, False),
-    ("store_y", 1, 1, 1, 0),
-    ("multiply", 2, 0, 2),
-    ("finish", 2, 0, 1, False),
-    ("interleave_y", 0, 1, 1),
-    ("quantize_psi", 3, 0),
-    ("store_y", 2, 0, 0, 0),
-    ("multiply", 2, 1, 1),
-    ("quantize_y", 1, 0),
-    ("quantize_u", 3, 0),
-    ("store_words", 1, 0, 0),
-    ("finish", 2, 1, 0, False),
-    ("quantize_y", 0, 1),
     ("multiply", 2, 0, 3),
-    ("interleave_y", 1, 1, 0),
-    ("store_words", 0, 1, 0),
-    ("finish", 2, 1, 1, False),
+    ("store_y", 1, 1, 1, 0),
+    ("finish", 2, 1, 0, False),
+    ("store_y", 2, 0, 0, 0),
+    ("interleave_y", 0, 1, 1),
+    ("multiply", 2, 0, 2),
+    ("quantize_psi", 3, 0),
+    ("multiply", 2, 1, 1),
+    ("finish", 2, 0, 3, False),
+    ("quantize_y", 1, 0),
     ("finish", 2, 0, 2, False),
     ("multiply", 2, 1, 3),
-    ("store_y", 2, 1, 0, 0),
     ("quantize_psi", 3, 1),
-    ("finish", 2, 0, 3, False),
-    ("quantize_u", 3, 1),
-    ("quantize_y", 1, 1),
-    ("multiply", 2, 1, 2),
-    ("finish", 2, 1, 3, False),
+    ("store_words", 1, 0, 0),
+    ("finish", 2, 1, 1, False),
     ("store_y", 2, 0, 1, 0),
-    ("interleave_y", 2, 0, 0),
-    ("store_words", 1, 1, 0),
-    ("multiply", 3, 0, 3),
-    ("finish", 2, 1, 2, False),
-    ("interleave_u", 4, 0, 2),
-    ("store_y", 2, 1, 1, 0),
-    ("multiply", 3, 0, 2),
-    ("finish", 3, 0, 3, False),
-    ("interleave_y", 2, 1, 0),
-    ("multiply", 3, 0, 0),
-    ("finish", 3, 0, 2, False),
-    ("quantize_y", 2, 0),
+    ("quantize_y", 0, 1),
     ("sine", 4, 0),
-    ("store_y", 3, 0, 1, 0),
-    ("interleave_u", 4, 1, 2),
-    ("store_words", 2, 0, 0),
+    ("quantize_u", 3, 0),
+    ("multiply", 2, 1, 2),
+    ("store_y", 2, 1, 0, 0),
+    ("store_words", 0, 1, 0),
+    ("interleave_y", 1, 1, 0),
+    ("finish", 2, 1, 3, False),
+    ("multiply", 3, 0, 0),
+    ("interleave_y", 2, 0, 0),
+    ("finish", 2, 1, 2, False),
     ("multiply", 3, 0, 1),
-    ("finish", 3, 0, 0, True),
-    ("times_amp", 4, 0),
-    ("multiply", 3, 1, 2),
-    ("finish", 3, 0, 1, False),
     ("sine", 4, 1),
+    ("store_y", 2, 1, 1, 0),
+    ("quantize_y", 1, 1),
+    ("quantize_y", 2, 0),
+    ("store_words", 1, 1, 0),
+    ("multiply", 3, 0, 2),
+    ("finish", 3, 0, 1, False),
+    ("interleave_y", 2, 1, 0),
+    ("store_words", 2, 0, 0),
+    ("finish", 3, 0, 0, False),
+    ("multiply", 3, 0, 3),
+    ("finish", 3, 0, 2, False),
+    ("interleave_u", 4, 0, 2),
+    ("times_amp", 4, 0),
     ("store_y", 3, 0, 0, 0),
-    ("quantize_y", 2, 1),
-    ("multiply", 3, 1, 3),
-    ("quantize_u", 4, 0),
-    ("store_scales", 0, 2, 0),
-    ("store_scales", 0, 3, 0),
-    ("store_words", 2, 1, 0),
+    ("multiply", 3, 1, 2),
+    ("interleave_u", 4, 1, 2),
+    ("finish", 3, 0, 3, False),
     ("times_amp", 4, 1),
-    ("store_scales", 0, 0, 0),
+    ("store_y", 3, 0, 1, 0),
+    ("multiply", 3, 1, 3),
+    ("finish", 3, 1, 2, False),
+    ("quantize_y", 2, 1),
     ("multiply", 3, 1, 1),
     ("finish", 3, 1, 3, False),
-    ("finish", 3, 1, 2, False),
-    ("quantize_psi", 4, 0),
-    ("multiply", 3, 1, 0),
     ("quantize_psi", 4, 1),
-    ("finish", 3, 1, 1, False),
-    ("store_y", 3, 1, 1, 0),
+    ("store_scales", 0, 2, 0),
+    ("quantize_psi", 4, 0),
+    ("store_scales", 0, 0, 0),
+    ("store_scales", 0, 3, 0),
+    ("store_words", 2, 1, 1),
     ("quantize_u", 4, 1),
-    ("store_scales", 0, 1, 0),
+    ("store_y", 3, 1, 1, 0),
+    ("quantize_u", 4, 0),
+    ("multiply", 3, 1, 0),
     ("interleave_y", 3, 0, 0),
-    ("multiply", 4, 0, 0),
-    ("finish", 3, 1, 0, False),
+    ("finish", 3, 1, 1, False),
+    ("store_scales", 0, 1, 1),
     ("multiply", 4, 0, 1),
-    ("finish", 4, 0, 0, False),
-    ("quantize_y", 3, 0),
-    ("store_y", 3, 1, 0, 0),
-    ("multiply", 4, 0, 2),
+    ("finish", 3, 1, 0, False),
+    ("multiply", 4, 0, 0),
     ("finish", 4, 0, 1, False),
     ("interleave_y", 3, 1, 0),
-    ("store_y", 4, 0, 0, 0),
+    ("store_y", 3, 1, 0, 0),
+    ("multiply", 4, 0, 2),
+    ("finish", 4, 0, 0, False),
     ("multiply", 4, 0, 3),
-    ("store_words", 3, 0, 0),
+    ("store_y", 4, 0, 0, 0),
     ("finish", 4, 0, 2, False),
+    ("quantize_y", 3, 0),
     ("multiply", 4, 1, 1),
     ("finish", 4, 0, 3, False),
-    ("store_y", 4, 0, 1, 0),
-    ("interleave_y", 4, 0, 0),
     ("multiply", 4, 1, 0),
-    ("finish", 4, 1, 1, False),
+    ("store_y", 4, 0, 1, 0),
+    ("finish", 4, 1, 1, True),
+    ("interleave_y", 4, 0, 1),
+    ("store_words", 3, 0, 0),
     ("quantize_y", 3, 1),
+    ("multiply", 4, 1, 3),
     ("multiply", 4, 1, 2),
-    ("finish", 4, 1, 0, False),
+    ("finish", 4, 1, 0, True),
+    ("store_words", 3, 1, 0),
+    ("finish", 4, 1, 3, True),
     ("store_y", 4, 1, 0, 0),
     ("quantize_y", 4, 0),
-    ("multiply", 4, 1, 3),
-    ("store_words", 3, 1, 0),
     ("finish", 4, 1, 2, False),
-    ("finish", 4, 1, 3, False),
-    ("store_words", 4, 0, 1),
-    ("store_y", 4, 1, 1, 0),
+    ("store_words", 4, 0, 0),
     ("interleave_y", 4, 1, 0),
+    ("store_y", 4, 1, 1, 0),
     ("quantize_y", 4, 1),
-    ("store_words", 4, 1, 1),
-    ("store_scales", 1, 3, 0),
-    ("store_scales", 1, 1, 0),
+    ("store_scales", 1, 0, 0),
+    ("store_scales", 1, 1, 1),
+    ("store_words", 4, 1, 0),
+    ("store_scales", 1, 3, 1),
     ("store_scales", 1, 2, 1),
-    ("store_scales", 1, 0, 1),
 ]
 
 

from contextlib import ExitStack

import concourse.mybir as mybir
from concourse.masks import make_identity

D, T, CH = 1024, 2048, 512
FLOPS = 2 * D * (D + CH) * T

F32 = mybir.dt.float32
BF16 = mybir.dt.bfloat16
U32 = mybir.dt.uint32
I32 = mybir.dt.int32
U8 = mybir.dt.uint8
FP8X4 = mybir.dt.float8_e4m3fn_x4
ACT = mybir.ActivationFunctionType
ALU = mybir.AluOpType

P = 128
PACK = 4
K_PASS = P * PACK
GROUPS = D // K_PASS
PSI_PASSES = D // K_PASS
U_PASS = PSI_PASSES
PASSES = PSI_PASSES + 1
BANKS = 7
BANK = 512
WIDTHS = [256, 512, 512, 512, 256]
STARTS = [sum(WIDTHS[:n]) for n in range(len(WIDTHS))]
CHUNKS = len(WIDTHS)
EARLY_CHUNKS = CHUNKS - 1
SCALE_STORES = [[0, 1, 2], [3, 4]]
LOADS = [[0], [1], [2], [3, 4]]
STORES = [[0], [1], [2], [3], [4]]
WORD_STORES = STORES
STORE_SLOTS = 2
UNITS = [(0,0),(1,0),(0,1),(1,1),(2,0),(2,1),(3,0),(3,1),(4,0),(4,1)]
W_USERS = [[("w", g, c, half) for half in range(2) for c in range(PASSES)] for g in range(GROUPS)]
Y_USERS = [[("y", n, g, t) for t in range(PACK)] for n, g in UNITS]
USERS = W_USERS[0] + Y_USERS[0] + W_USERS[1] + sum(Y_USERS[1:], [])
SORTED = []
SORT_BUFS = 3
SIN_BUFS, PSI_BUFS, U_BUFS, YB_BUFS, X_BUFS, W_BUFS = 3, 3, 2, 2, 3, 3


def span(chunks):
    return slice(STARTS[chunks[0]], STARTS[chunks[-1]] + WIDTHS[chunks[-1]])


def place(groups, n):
    for j, chunks in enumerate(groups):
        if n in chunks:
            first = STARTS[n] - STARTS[chunks[0]]
            return j, slice(first, first + WIDTHS[n])


def width(chunks):
    return sum(WIDTHS[n] for n in chunks)


ORDER = [
    ("load_koopman", 0, 0),
    ("prepare",),
    ("load_amp",),
    ("load_phases", 0, 0),
    ("load_phases", 0, 1),
    ("load_koopman", 0, 1),
    ("load_phases", 1, 0),
    ("load_control", 0),
    ("load_koopman", 1, 0),
    ("turn_weight", 0, 1, 0),
    ("load_u", 0),
    ("load_phases", 1, 1),
    ("sort_vectors",),
    ("load_control", 1),
    ("sine", 0, 0),
    ("load_unit",),
    ("copy_weight", 0, 1, 0, True),
    ("load_u", 1),
    ("turn_weight", 0, 0, 0),
    ("affine",),
    ("sine", 0, 1),
    ("times_amp", 0, 0),
    ("load_phases", 2, 0),
    ("turn_weight", 0, 1, 1),
    ("copy_weight", 0, 0, 0, False),
    ("times_amp", 0, 1),
    ("load_koopman", 1, 1),
    ("sine", 1, 0),
    ("turn_weight", 0, 0, 1),
    ("load_u", 3),
    ("quantize_psi", 0, 0),
    ("copy_weight", 0, 1, 1, True),
    ("turn_weight", 0, 2, 0),
    ("quantize_psi", 0, 1),
    ("load_phases", 2, 1),
    ("quantize_weight", 0, 1),
    ("turn_weight", 0, 2, 1),
    ("load_phases", 3, 0),
    ("copy_weight", 0, 2, 0, False),
    ("times_amp", 1, 0),
    ("interleave_u", 0, 0, 2),
    ("copy_weight", 0, 0, 1, False),
    ("turn_weight", 1, 1, 0),
    ("interleave_u", 0, 1, 2),
    ("copy_weight", 0, 2, 1, False),
    ("load_u", 2),
    ("sine", 1, 1),
    ("turn_weight", 1, 0, 0),
    ("load_phases", 3, 1),
    ("quantize_u", 0, 0),
    ("quantize_weight", 0, 0),
    ("turn_weight", 1, 2, 0),
    ("quantize_weight", 0, 2),
    ("quantize_u", 0, 1),
    ("quantize_psi", 1, 0),
    ("multiply", 0, 0, 2),
    ("copy_weight", 1, 2, 0, False),
    ("copy_weight", 1, 0, 0, True),
    ("interleave_u", 1, 1, 2),
    ("multiply", 0, 0, 1),
    ("finish", 0, 0, 2, False),
    ("times_amp", 1, 1),
    ("multiply", 0, 0, 0),
    ("finish", 0, 0, 1, False),
    ("sine", 2, 0),
    ("multiply", 0, 0, 3),
    ("interleave_u", 1, 0, 2),
    ("turn_weight", 1, 1, 1),
    ("turn_weight", 1, 2, 1),
    ("finish", 0, 0, 0, True),
    ("copy_weight", 1, 1, 1, True),
    ("quantize_psi", 1, 1),
    ("turn_weight", 1, 0, 1),
    ("copy_weight", 1, 2, 1, False),
    ("quantize_u", 1, 1),
    ("copy_weight", 1, 1, 0, False),
    ("quantize_u", 1, 0),
    ("quantize_weight", 1, 2),
    ("multiply", 1, 0, 3),
    ("copy_weight", 1, 0, 1, False),
    ("quantize_weight", 1, 1),
    ("finish", 0, 0, 3, False),
    ("multiply", 1, 0, 2),
    ("sine", 2, 1),
    ("quantize_weight", 1, 0),
    ("store_y", 0, 0, 1, 0),
    ("store_y", 0, 0, 0, 0),
    ("finish", 1, 0, 3, True),
    ("interleave_y", 0, 0, 2),
    ("multiply", 1, 0, 1),
    ("times_amp", 2, 0),
    ("interleave_u", 2, 0, 2),
    ("multiply", 0, 1, 0),
    ("finish", 1, 0, 2, False),
    ("multiply", 0, 1, 1),
    ("finish", 1, 0, 1, False),
    ("store_y", 1, 0, 1, 0),
    ("multiply", 1, 0, 0),
    ("finish", 0, 1, 0, False),
    ("interleave_u", 2, 1, 2),
    ("finish", 0, 1, 1, True),
    ("times_amp", 2, 1),
    ("store_y", 0, 1, 0, 0),
    ("multiply", 0, 1, 2),
    ("finish", 1, 0, 0, False),
    ("multiply", 1, 1, 0),
    ("sine", 3, 0),
    ("store_y", 1, 0, 0, 0),
    ("multiply", 0, 1, 3),
    ("multiply", 1, 1, 1),
    ("quantize_y", 0, 0),
    ("quantize_u", 2, 0),
    ("store_words", 0, 0, 0),
    ("quantize_u", 2, 1),
    ("quantize_psi", 2, 1),
    ("finish", 0, 1, 3, False),
    ("multiply", 1, 1, 2),
    ("finish", 0, 1, 2, False),
    ("interleave_u", 3, 1, 0),
    ("finish", 1, 1, 1, False),
    ("store_y", 0, 1, 1, 0),
    ("multiply", 1, 1, 3),
    ("quantize_psi", 2, 0),
    ("finish", 1, 1, 0, False),
    ("sine", 3, 1),
    ("quantize_u", 3, 1),
    ("store_y", 1, 1, 0, 0),
    ("times_amp", 3, 0),
    ("interleave_u", 3, 0, 2),
    ("multiply", 2, 0, 1),
    ("multiply", 2, 0, 0),
    ("interleave_y", 1, 0, 2),
    ("finish", 1, 1, 3, False),
    ("multiply", 2, 1, 0),
    ("finish", 2, 0, 1, True),
    ("finish", 1, 1, 2, False),
    ("times_amp", 3, 1),
    ("finish", 2, 0, 0, False),
    ("multiply", 2, 0, 3),
    ("store_y", 1, 1, 1, 0),
    ("finish", 2, 1, 0, False),
    ("store_y", 2, 0, 0, 0),
    ("interleave_y", 0, 1, 1),
    ("multiply", 2, 0, 2),
    ("quantize_psi", 3, 0),
    ("multiply", 2, 1, 1),
    ("finish", 2, 0, 3, False),
    ("quantize_y", 1, 0),
    ("finish", 2, 0, 2, False),
    ("multiply", 2, 1, 3),
    ("quantize_psi", 3, 1),
    ("store_words", 1, 0, 0),
    ("finish", 2, 1, 1, False),
    ("store_y", 2, 0, 1, 0),
    ("quantize_y", 0, 1),
    ("sine", 4, 0),
    ("quantize_u", 3, 0),
    ("multiply", 2, 1, 2),
    ("store_y", 2, 1, 0, 0),
    ("store_words", 0, 1, 0),
    ("interleave_y", 1, 1, 0),
    ("finish", 2, 1, 3, False),
    ("multiply", 3, 0, 0),
    ("interleave_y", 2, 0, 0),
    ("finish", 2, 1, 2, False),
    ("multiply", 3, 0, 1),
    ("sine", 4, 1),
    ("store_y", 2, 1, 1, 0),
    ("quantize_y", 1, 1),
    ("quantize_y", 2, 0),
    ("store_words", 1, 1, 0),
    ("multiply", 3, 0, 2),
    ("finish", 3, 0, 1, False),
    ("interleave_y", 2, 1, 0),
    ("store_words", 2, 0, 0),
    ("finish", 3, 0, 0, False),
    ("multiply", 3, 0, 3),
    ("finish", 3, 0, 2, False),
    ("interleave_u", 4, 0, 2),
    ("times_amp", 4, 0),
    ("store_y", 3, 0, 0, 0),
    ("multiply", 3, 1, 2),
    ("interleave_u", 4, 1, 2),
    ("finish", 3, 0, 3, False),
    ("times_amp", 4, 1),
    ("store_y", 3, 0, 1, 0),
    ("multiply", 3, 1, 3),
    ("finish", 3, 1, 2, False),
    ("quantize_y", 2, 1),
    ("multiply", 3, 1, 1),
    ("finish", 3, 1, 3, False),
    ("quantize_psi", 4, 1),
    ("store_scales", 0, 2, 0),
    ("quantize_psi", 4, 0),
    ("store_scales", 0, 0, 0),
    ("store_scales", 0, 3, 0),
    ("store_words", 2, 1, 1),
    ("quantize_u", 4, 1),
    ("store_y", 3, 1, 1, 0),
    ("quantize_u", 4, 0),
    ("multiply", 3, 1, 0),
    ("interleave_y", 3, 0, 0),
    ("finish", 3, 1, 1, False),
    ("store_scales", 0, 1, 1),
    ("multiply", 4, 0, 1),
    ("finish", 3, 1, 0, False),
    ("multiply", 4, 0, 0),
    ("finish", 4, 0, 1, False),
    ("interleave_y", 3, 1, 0),
    ("store_y", 3, 1, 0, 0),
    ("multiply", 4, 0, 2),
    ("finish", 4, 0, 0, False),
    ("multiply", 4, 0, 3),
    ("store_y", 4, 0, 0, 0),
    ("finish", 4, 0, 2, False),
    ("quantize_y", 3, 0),
    ("multiply", 4, 1, 1),
    ("finish", 4, 0, 3, False),
    ("multiply", 4, 1, 0),
    ("store_y", 4, 0, 1, 0),
    ("finish", 4, 1, 1, True),
    ("interleave_y", 4, 0, 1),
    ("store_words", 3, 0, 0),
    ("quantize_y", 3, 1),
    ("multiply", 4, 1, 3),
    ("multiply", 4, 1, 2),
    ("finish", 4, 1, 0, True),
    ("store_words", 3, 1, 0),
    ("finish", 4, 1, 3, True),
    ("store_y", 4, 1, 0, 0),
    ("quantize_y", 4, 0),
    ("finish", 4, 1, 2, False),
    ("store_words", 4, 0, 0),
    ("interleave_y", 4, 1, 0),
    ("store_y", 4, 1, 1, 0),
    ("quantize_y", 4, 1),
    ("store_scales", 1, 0, 0),
    ("store_scales", 1, 1, 1),
    ("store_words", 4, 1, 0),
    ("store_scales", 1, 3, 1),
    ("store_scales", 1, 2, 1),
]


def tile_koopman_control_step_g2_kernel(tc, phases, amp, koopman, control, u, drift, unit, out_0, out_1, out_2):
    nc = tc.nc
    with ExitStack() as ctx:
        keep = ctx.enter_context(tc.tile_pool(name="keep", bufs=1))
        psum = ctx.enter_context(tc.psum_pool(name="psum", bufs=1))
        ctx.enter_context(tc.manual_schedule())

        def ring(name, count, shape, dtype):
            return [keep.tile(shape, dtype, name="%s%d" % (name, j), align_bytes=64) for j in range(count)]

        banks = [psum.tile([P, BANK], F32, name="bank%d" % j) for j in range(BANKS)]
        ident = keep.tile([P, P], F32, name="ident")
        zero = keep.tile([P, 1], F32, name="zero")
        zero_bias = keep.tile([P, 1], F32, name="zero_bias")
        ident_bf = keep.tile([P, P], BF16, name="ident_bf")
        vec_rows = keep.tile([P, K_PASS], BF16, name="vec_rows")
        vec_sorted = keep.tile([P, PACK, P], BF16, name="vec_sorted")
        vecs = psum.tile([P, PACK, P], BF16, name="vecs")
        unit32 = keep.tile([P, PACK, GROUPS], F32, name="unit32")
        bias32 = keep.tile([P, PACK, GROUPS], F32, name="bias32")

        ph_raw = [[keep.tile([P, PACK, width(ns)], BF16, name="ph%d_%d" % (j, c)) for c in range(PSI_PASSES)] for j, ns in enumerate(LOADS)]
        u_raw = [keep.tile([P, PACK, width(ns)], BF16, name="u%d" % j) for j, ns in enumerate(LOADS)]
        sin32 = ring("sin", SIN_BUFS, [P, PACK, BANK], F32)
        psi_bf = ring("psi_bf", PSI_BUFS, [P, PACK * BANK], BF16)
        u_bf = ring("u_bf", 2, [P, PACK * BANK // 2], BF16)
        y32 = [ring("y32_%d_" % j, GROUPS, [P, PACK, width(ns)], F32) for j, ns in enumerate(STORES)]
        y_bf = ring("y_bf", YB_BUFS, [P, PACK * BANK], BF16)
        w_bf = ring("w_bf", W_BUFS, [P, PACK * K_PASS], BF16)
        koop_raw, ctl_raw = y32[-2], y32[-1]
        w_sorted = ring("w_sorted", SORT_BUFS, [P, 2, 2, P], F32)
        x_code_ring = [ring("xc%d_" % j, PASSES, [P, BANK], U32) for j in range(X_BUFS)]
        x_scale_ring = [ring("xs%d_" % j, PASSES, [P, BANK], U8) for j in range(X_BUFS)]
        x_codes = [[x_code_ring[n % X_BUFS][c][:, :w] for c in range(PASSES)] for n, w in enumerate(WIDTHS)]
        x_scales = [[x_scale_ring[n % X_BUFS][c][:, :w] for c in range(PASSES)] for n, w in enumerate(WIDTHS)]
        w_codes = [ring("wc%d_" % g, PASSES, [P, K_PASS], U32) for g in range(GROUPS)]
        w_scales = [ring("ws%d_" % g, PASSES, [P, K_PASS], U8) for g in range(GROUPS)]
        y_codes = [ring("yc%d_" % j, GROUPS, [P, width(ns)], U32) for j, ns in enumerate(WORD_STORES)]
        y_scales = [keep.tile([P, width(ns)], U8, name="ys%d" % j, align_bytes=64) for j, ns in enumerate(SCALE_STORES)]

        words_out = out_1.rearrange("g p m t -> g p (m t)").bitcast(I32)
        scales_out = out_2.bitcast(I32)

        queues = [nc.sync, nc.scalar]

        def cols(n):
            return slice(STARTS[n], STARTS[n] + WIDTHS[n])

        def rows(c):
            return slice(c * K_PASS, (c + 1) * K_PASS)

        def load_vector(row, src):
            nc.sync.dma_start(out=vec_rows[row : row + GROUPS, :], in_=src.rearrange("(g k) -> g k", g=GROUPS))

        def load_phases(j, c):
            nc.sync.dma_start(out=ph_raw[j][c][:], in_=phases[rows(c), span(LOADS[j])].rearrange("(p t) m -> p t m", t=PACK))

        def load_u(j):
            nc.sync.dma_start(out=u_raw[j][:], in_=u[:, span(LOADS[j])].rearrange("(p t) m -> p t m", t=PACK))

        def load_koopman(g, half):
            slots = slice(2 * half, 2 * half + 2)
            nc.sync.dma_start(out=koop_raw[g][:, slots, :].bitcast(BF16), in_=koopman[rows(g), :].rearrange("(p t) k -> p t k", t=PACK)[:, slots, :])

        def load_control(g):
            nc.sync.dma_start(out=ctl_raw[g][:].bitcast(BF16), in_=control[rows(g), :].rearrange("(p t) k -> p t k", t=PACK))

        def interleaved(tile_bf, w, run):
            return tile_bf[:, : PACK * w].rearrange("p (b i t) -> p b t i", i=run, t=PACK)

        def by_slot(tile, run):
            return tile.rearrange("p t (b i) -> p b t i", i=run)

        def interleave(dst, src, engine):
            if engine == 0:
                nc.vector.tensor_copy(out=dst, in_=src)
            elif engine == 1:
                nc.scalar.copy(out=dst, in_=src)
            else:
                nc.gpsimd.tensor_scalar(out=dst, in0=src, scalar1=1.0, scalar2=0.0, op0=ALU.mult, op1=ALU.add)

        def quantize(codes, scales, src):
            nc.vector.quantize_mx(out=codes.bitcast(FP8X4), scales=scales, in_=src)

        def sine(n, c):
            group, inside = place(LOADS, n)
            j = PSI_PASSES * n + c
            nc.scalar.activation(out=sin32[j % SIN_BUFS][:, :, : WIDTHS[n]], in_=ph_raw[group][c][:, :, inside], func=ACT.Sin, bias=zero_bias[:])

        def times_amp(n, c):
            j, w = PSI_PASSES * n + c, WIDTHS[n]
            factor = vecs[:, :, c : c + 1].unsqueeze(1).to_broadcast([P, w // 4, PACK, 4])
            nc.vector.tensor_tensor(out=interleaved(psi_bf[j % PSI_BUFS], w, 4), in0=by_slot(sin32[j % SIN_BUFS][:, :, :w], 4), in1=factor, op=ALU.mult)

        def quantize_psi(n, c):
            j = PSI_PASSES * n + c
            quantize(x_codes[n][c], x_scales[n][c], psi_bf[j % PSI_BUFS][:, : PACK * WIDTHS[n]])

        def interleave_u(n, half, engine):
            group, inside = place(LOADS, n)
            w = WIDTHS[n] // 2
            src = u_raw[group][:, :, inside][:, :, half * w : (half + 1) * w]
            interleave(interleaved(u_bf[half], w, 4), by_slot(src, 4), engine)

        def quantize_u(n, half):
            w = WIDTHS[n] // 2
            part = slice(half * w, (half + 1) * w)
            quantize(x_codes[n][U_PASS][:, part], x_scales[n][U_PASS][:, part], u_bf[half][:, : PACK * w])

        def weight_words(g, c, half):
            src = ctl_raw[g][:] if c == U_PASS else koop_raw[g][:, :, c * K_PASS // 2 : (c + 1) * K_PASS // 2]
            return src[:, 2 * half : 2 * half + 2, :]

        def sort_weight(g, c, half, on_scalar):
            dst = w_sorted[SORTED.index(("w", g, c, half)) % SORT_BUFS][:]
            src = weight_words(g, c, half).rearrange("p s (q e) -> p s e q", e=2)
            if on_scalar:
                nc.scalar.copy(out=dst, in_=src)
            else:
                nc.vector.tensor_copy(out=dst, in_=src)

        def turn_weight(g, c, half):
            bank = banks[USERS.index(("w", g, c, half)) % BANKS]
            for s in range(2):
                for e in range(2):
                    at = (2 * s + e) * P
                    if ("w", g, c, half) in SORTED:
                        src = w_sorted[SORTED.index(("w", g, c, half)) % SORT_BUFS][:, s, e, :]
                    else:
                        src = weight_words(g, c, half)[:, s, e::2]
                    nc.tensor.transpose(bank[:, at : at + P], src, ident[:])

        def copy_weight(g, c, half, on_vector=False):
            bank = banks[USERS.index(("w", g, c, half)) % BANKS]
            dst = w_bf[(g * PASSES + c) % W_BUFS][:].bitcast(F32)[:, half * BANK : (half + 1) * BANK]
            dst, src = dst.rearrange("p (s m e) -> p s m e", s=2, e=2), bank[:].rearrange("p (s e m) -> p s m e", s=2, e=2)
            if on_vector:
                nc.vector.tensor_copy(out=dst, in_=src)
            else:
                nc.scalar.copy(out=dst, in_=src)

        def quantize_weight(g, c):
            quantize(w_codes[g][c][:], w_scales[g][c][:], w_bf[(g * PASSES + c) % W_BUFS][:])

        def acc_bank(n, g, t):
            return banks[USERS.index(("y", n, g, t)) % BANKS][:, : WIDTHS[n]]

        def multiply(n, g, t):
            m = slice(t * P, (t + 1) * P)
            for c in range(PASSES):
                nc.tensor.matmul_mx(
                    out=acc_bank(n, g, t),
                    lhsT=w_codes[g][c][:, m].bitcast(FP8X4),
                    lhsT_scale=w_scales[g][c][:, m],
                    rhs=x_codes[n][c].bitcast(FP8X4),
                    rhs_scale=x_scales[n][c],
                    start=(c == 0),
                    stop=(c == PASSES - 1),
                )

        def y_tile(n, g):
            group, inside = place(STORES, n)
            return y32[group][g][:, :, inside]

        def finish(n, g, t, on_vector=False):
            dst = y_tile(n, g)[:, t, :]
            scale, bias = unit32[:, t, g : g + 1], bias32[:, t, g : g + 1]
            if on_vector:
                nc.vector.tensor_scalar(out=dst, in0=acc_bank(n, g, t), scalar1=scale, scalar2=bias, op0=ALU.mult, op1=ALU.add)
            else:
                nc.scalar.activation(out=dst, in_=acc_bank(n, g, t), func=ACT.Identity, bias=bias, scale=scale)

        def store_y(j, g, part, queue):
            slots = slice(part * STORE_SLOTS, (part + 1) * STORE_SLOTS)
            queues[queue].dma_start(out=out_0[rows(g), span(STORES[j])].rearrange("(p t) m -> p t m", t=PACK)[:, slots, :], in_=y32[j][g][:, slots, :])

        def interleave_y(n, g, engine):
            w = WIDTHS[n]
            interleave(interleaved(y_bf[UNITS.index((n, g)) % YB_BUFS], w, 4), by_slot(y_tile(n, g), 4), engine)

        def quantize_y(n, g):
            group, inside = place(SCALE_STORES, n)
            scales = y_scales[group][4 * g :, inside]
            group, inside = place(WORD_STORES, n)
            quantize(y_codes[group][g][:, inside], scales, y_bf[UNITS.index((n, g)) % YB_BUFS][:, : PACK * WIDTHS[n]])

        def store_words(j, g, queue):
            queues[queue].dma_start(out=words_out[g, :, span(WORD_STORES[j])], in_=y_codes[j][g][:].bitcast(I32))

        def store_scales(j, q, queue):
            columns = span(SCALE_STORES[j])
            queues[queue].dma_start(
                out=scales_out[:, 4 * q : 4 * q + 4, columns.start // 4 : columns.stop // 4],
                in_=y_scales[j][32 * q : 32 * q + 8, :].bitcast(I32),
            )

        def prepare():
            nc.vector.memset(zero[:], 0.0)
            nc.scalar.activation(out=zero_bias[:], in_=zero[:], func=ACT.Sin)
            nc.vector.memset(vec_rows[:], 0.0)
            make_identity(nc, ident[:])
            nc.vector.tensor_copy(out=ident_bf[:], in_=ident[:])

        def load_amp():
            load_vector(0, amp)
            load_vector(2, unit)
            load_vector(4, drift)

        def sort_vectors():
            nc.vector.tensor_copy(out=vec_sorted[:], in_=vec_rows[:].rearrange("r (p t) -> r t p", t=PACK))

        def load_unit():
            for t in range(PACK):
                nc.tensor.transpose(vecs[:, t, :], vec_sorted[:, t, :], ident_bf[:])

        def affine():
            nc.vector.tensor_copy(out=unit32[:], in_=vecs[:, :, 2:4])
            nc.vector.tensor_tensor(out=bias32[:], in0=vecs[:, :, 4:6], in1=unit32[:], op=ALU.mult)

        steps = dict(
            prepare=prepare, load_amp=load_amp, load_unit=load_unit, affine=affine, store_scales=store_scales,
            load_phases=load_phases, load_u=load_u, load_koopman=load_koopman, load_control=load_control, sine=sine, times_amp=times_amp, quantize_psi=quantize_psi,
            interleave_u=interleave_u, quantize_u=quantize_u, turn_weight=turn_weight, sort_weight=sort_weight, sort_vectors=sort_vectors, copy_weight=copy_weight,
            quantize_weight=quantize_weight, multiply=multiply, finish=finish, store_y=store_y, interleave_y=interleave_y,
            quantize_y=quantize_y, store_words=store_words,
        )
        for name, *args in ORDER:
            steps[name](*args)
